import numpy as np, ml_dtypes
CORES = [2,6,10,14,18,22,26,30]
N = 8
import mx_ref
BF = ml_dtypes.bfloat16
def cols(t, e):
    v = np.concatenate([t.reshape(128, -1, 4), np.zeros((128, 1, 4), BF)], axis=1)
    return np.ascontiguousarray(v[:, e]).reshape(128, -1)
def tile(rs):
    return np.stack(rs, axis=2).reshape(128, -1).astype(BF)
def cut(t, i, w=512):
    return t[:, w * i:w * i + w]
def f(rng, *shape):
    return mx_ref.flush((rng.standard_normal(shape, dtype=np.float32) * np.exp2(rng.integers(-2, 3, shape[:-1] + (1,)))).astype(BF))
def wide(rng, *shape, cols=0):
    v = rng.standard_normal(shape, dtype=np.float32) * np.exp2(rng.integers(-12, 13, shape)).astype(np.float32)
    if cols: v *= np.repeat(np.exp2(rng.integers(-cols, cols + 1, shape[:-2] + (1, shape[-1] // 4))) * (rng.random(shape[:-2] + (1, shape[-1] // 4)) > 0.0625), 4, axis=-1).astype(np.float32)
    return mx_ref.flush(v.astype(BF))
T, ST = 512, 128
def flags(rng, n, new):
    s = np.zeros((N, T), bool)
    for r in range(N):
        s[r, 0] = new[r] > 0
        s[r, 1 + rng.permutation(T - 1)[:int(n[r]) - int(new[r])]] = True
    return s
def borders(rng):
    new = rng.integers(0, 2, N); new[0] = 1
    return new
def make(rng, s, far=2, spread=False):
    t = np.zeros((128, 128, 4), np.float32); t[:, :16] = rng.standard_normal((128, 16, 4), dtype=np.float32)
    if spread: t[64:] = 0
    t = mx_ref.flush(t.reshape(128, 512).astype(BF))
    k = (rng.integers(0, 16) + np.cumsum(s.reshape(-1) * rng.integers(1, 16, N * T))) % 16
    c = t.astype(np.float32).reshape(128, 128, 4)[:, k] + rng.standard_normal((128, N * T, 4), dtype=np.float32) * np.float32(0.125)
    if spread: c[64:] = wide(rng, 64, 4 * N * T).astype(np.float32).reshape(64, N * T, 4)
    c = c * np.exp2(rng.integers(-far, far + 1, (N * T, 1))).astype(np.float32)
    x = np.ascontiguousarray(c.reshape(128, N, 4 * T).transpose(1, 0, 2)).astype(BF)
    return {"x": mx_ref.flush(x), "p": np.stack([t] * N), "a": f(rng, N, 128, 2048), "w": f(rng, N, 128, 512), "v": f(rng, N, 128, 512)}
def setup_inputs(rng):
    return make(rng, flags(rng, rng.integers(1, ST + 1, N), borders(rng)))
def setup_inputs_border(rng):
    return make(rng, flags(rng, rng.integers(1, ST + 1, N), np.arange(N) == 0))
def setup_inputs_dense(rng):
    n = np.full(N, ST); n[0] = ST - rng.integers(1, N)
    return make(rng, flags(rng, n, borders(rng)))
def setup_inputs_one(rng):
    return make(rng, flags(rng, np.ones(N, int), np.arange(N) == 0))
def setup_inputs_spread(rng):
    return make(rng, flags(rng, rng.integers(1, ST + 1, N), borders(rng)), far=8, spread=True)
def setup_inputs_ties(rng):
    d = setup_inputs(rng)
    m = np.cumsum(flags(rng, rng.integers(1, ST + 1, N), borders(rng)).reshape(-1)) - 1; n = int(m[-1]) + 1
    u = np.zeros((128, 8, 4), np.float32); u[:64] = rng.choice([-1, 1], (64, 8, 4)) * rng.uniform(0.75, 1.25, (64, 8, 4))
    g = np.zeros((128, 1, 4), np.float32); g[64:] = rng.choice([-1, 1], (64, 1, 4))
    t = np.zeros((128, 128, 4), np.float32); t[:, :8] = u + g; t[:, 8:16] = u + g
    k = np.cumsum(rng.integers(1, 8, n)) % 8
    big = int(np.argmax(np.bincount(m)))
    k = (k - k[big]) % 8
    neg = rng.permutation(n) % 2
    c = u[:, k[m]] + g * np.where(neg[m] > 0, -2, 1).astype(np.float32)[:, None] + rng.standard_normal((128, N * T, 4), dtype=np.float32) * np.float32(0.125)
    c = c * np.exp2(rng.integers(-2, 3, (N * T, 1))).astype(np.float32)
    zero = (k[m] == 0) & (rng.random(N * T) < 0.25); zero[np.flatnonzero(m == big)[1]] = True
    c[:, zero] = 0
    d["x"] = mx_ref.flush(np.ascontiguousarray(c.reshape(128, N, 4 * T).transpose(1, 0, 2)).astype(BF))
    d["p"] = np.stack([mx_ref.flush(t.reshape(128, 512).astype(BF))] * N)
    return d
def labels(x, p):
    return np.stack([np.argmax(mx_ref.matmul(mx_ref.quantize(p[r]), mx_ref.quantize(x[r]))[:16] + np.float32(0.0), axis=0) for r in range(N)])
def starts(l):
    e = l.reshape(-1)
    return np.concatenate([[True], e[1:] != e[:-1]])
def check_inputs(d):
    b = []
    for r in range(N):
        if not np.array_equal(d["p"][r], d["p"][0]): b.append("p (the same on all ranks)")
        if d["p"][r][:, 64:].astype(np.float32).any(): b.append("p (zero columns)")
    n = starts(labels(d["x"], d["p"])).reshape(N, T).sum(axis=1)
    if n.min() < 1 or n.max() > ST: b.append("x (runs that start on a rank)")
    return b
def reference(x, p, a, w, v):
    l = labels(x, p); s = starts(l)
    m = np.add.accumulate(s.astype(int)) - 1
    first = np.flatnonzero(s)
    seq = np.concatenate([x[r] for r in range(N)], axis=1)
    h = []
    for r in range(N):
        e = np.full(ST, -1); mine = first[r::N]; e[:len(mine)] = mine
        c = mx_ref.quantize(cols(seq, e))
        h.append(tile([np.maximum(mx_ref.matmul(mx_ref.quantize(np.ascontiguousarray(cut(a[r], i))), c), np.float32(0)) * np.float32(0.05) for i in range(4)]))
    h = np.concatenate(h, axis=1)
    y = np.zeros((N, 128, T), np.float32); lb = np.zeros((N, 2, T), np.float32)
    for r in range(N):
        k = m[r * T:r * T + T]
        hk = mx_ref.quantize(cols(h, (k % N) * ST + k // N))
        y[r] = mx_ref.matmul(mx_ref.quantize(w[r]), mx_ref.quantize(x[r])) + mx_ref.matmul(mx_ref.quantize(v[r]), hk)
        lb[r, 0] = l[r]; lb[r, 1] = k
    return {"y": y, "lb": lb}

@@ -1,0 +1,360 @@
+from concourse.bass import DstId, RemoteDMATransfer
+from concourse.mybir import dt, AluOpType, AxisListType, ActivationFunctionType
+
+N = 8
+S = 18
+NC = N * S
+FW = 160 + 512
+
+F32, BF, I32, U16, C8, U8 = "float32", "bfloat16", "int32", "uint16", "float8_e4m3fn_x4", "uint8"
+
+
+def _sb(n, d):
+    return ("sbuf", [128, n], d)
+
+
+SCRATCH = {
+    "ps": ("psum", [128, 4096], F32),
+    "xs": _sb(2048, BF), "pt": _sb(576, BF), "at": _sb(2048, BF), "wt": _sb(512, BF), "vt": _sb(512, BF),
+    "qx": _sb(512, C8), "sx": _sb(512, U8), "qp": _sb(144, C8), "sp": _sb(144, U8),
+    "qa": _sb(512, C8), "sa": _sb(512, U8), "qw": _sb(128, C8), "sw": _sb(128, U8), "qv": _sb(128, C8), "sv": _sb(128, U8),
+    "ct": _sb(592, BF), "qc": _sb(NC + 126, C8), "sc": _sb(NC + 126, U8),
+    "ht": _sb(576, BF), "qh": _sb(NC + 126, C8), "sh": _sb(NC + 126, U8),
+    "pi": _sb(1, I32), "pj": _sb(4, I32), "pf": _sb(4, F32), "j4i": _sb(32, I32), "j4m": _sb(32, I32), "j4": _sb(32, F32),
+    "trash": _sb(32, F32), "val": _sb(512, F32), "prmi": _sb(8, I32), "prm": _sb(8, U16), "ypi": _sb(128, I32),
+    "msk": _sb(128, F32), "d0": _sb(128, F32), "c1": _sb(1, F32), "c2": _sb(1, F32), "c3": _sb(1, F32), "rst": _sb(2, F32),
+    "reset": _sb(256, F32), "one2": _sb(256, BF), "one": _sb(32, F32), "k256": _sb(32, F32),
+    "z": _sb(288, F32), "mx": _sb(256, F32), "nn": _sb(256, BF), "ss": _sb(256, BF), "gg": _sb(64, F32), "h2": _sb(64, F32),
+    "fl": _sb(32, F32), "cs": _sb(32, F32), "z1": _sb(1, F32), "z2": _sb(1, F32), "dm": _sb(32, F32), "dmt": _sb(32, F32),
+    "enc": _sb(1, F32), "e16": _sb(2, U16), "owni": _sb(1, I32),
+    "fj": _sb(32, F32), "lj": _sb(1, F32), "dm2": _sb(64, F32), "dm2t": _sb(64, F32), "last": _sb(1, F32),
+    "lastl": _sb(2, U16), "iw": _sb(32, F32), "ex": _sb(32, F32), "nfe": _sb(32, F32), "nfd": _sb(64, F32),
+    "cd": _sb(64, F32), "od": _sb(64, F32), "to": _sb(64, F32), "offl": _sb(32, U16), "ff": _sb(FW, F32),
+    "mk": _sb(128, F32), "sg": _sb(128, F32), "uu": _sb(32, F32),
+    "m16": _sb(8, U16), "mi": _sb(8, I32), "fi": _sb(8, I32), "la": _sb(8, I32), "ci": _sb(8, I32), "ne": _sb(8, I32),
+    "dd": _sb(8, F32), "bb": _sb(1, F32), "nf0": _sb(1, F32), "ri": _sb(2, I32), "ra": _sb(2, I32), "ro": _sb(2, U16),
+    "lst": _sb(32, U16),
+    "tc": _sb(64, F32), "ii": _sb(64, I32), "t1": _sb(64, I32), "kk": _sb(64, I32), "k18": _sb(64, F32), "fx": _sb(64, F32),
+    "s1": _sb(64, F32), "s2": _sb(64, F32), "fin": _sb(32, U16), "lb0": _sb(32, F32), "lb1": _sb(32, F32),
+    "wx": _sb(512, F32), "vw": _sb(NC, F32), "yt": _sb(512, F32),
+}
+SEMAPHORES = ["kv", "ks", "kt", "kg", "dp", "dx0", "dx1", "dx2", "dx3", "da", "dw", "dv", "dy0", "dy1", "dl0", "dl1",
+              "e0", "e1", "e2", "l0", "l1", "l2"]
+
+
+def _mask(es):
+    return sum(1 << e for e in es)
+
+
+def _near(core, d, off_engines, topo):
+    return [e for e in topo.engines(core, d) if e not in off_engines][:2]
+
+
+def _plan(core, cores, topo):
+    ch = topo.chip(core)
+    off = [d for d in cores if topo.chip(d) != ch]
+    off.sort(key=lambda d: (0 if topo.mates(ch, topo.chip(d)) else 1 if topo.same_plane(ch, topo.chip(d)) else 2, d))
+    eo = topo.engines(core, off[0])
+    plan = {}
+    for i, d in enumerate(off):
+        j = 2 * (i - 4)
+        plan[d] = ([eo[i]], [eo[4 + i]]) if i < 4 else (eo[4 + j:6 + j], eo[j:j + 2])
+    for d in cores:
+        if d != core and topo.chip(d) == ch:
+            plan[d] = (_near(core, d, eo, topo),) * 2
+    return plan
+
+
+def _plan0(core, cores, topo):
+    ch = topo.chip(core)
+    eo = [topo.engines(core, d) for d in cores if topo.chip(d) != ch][0]
+    return {d: eo if topo.chip(d) != ch else _near(core, d, eo, topo) for d in cores[cores.index(core) + 1:]}
+
+
+def rank_program(g, core, T, topo):
+    r = T.rank_of(core)
+    if r is None:
+        return
+    A, X, AF = AluOpType, AxisListType.X, ActivationFunctionType
+    cores = list(T.cores)
+    vec, sca, ten, syn = g.vector, g.scalar, g.tensor, g.sync
+    queue = {"v": vec, "s": sca, "t": ten, "g": g, "y": syn}
+    cnt, known = {}, {}
+
+    def done(ins, sem, n=1):
+        ins.then_inc(T.sem[sem], n)
+        cnt[sem] = cnt.get(sem, 0) + n
+        return (sem, cnt[sem])
+
+    def need(qn, *toks):
+        for s, v in toks:
+            if known.get((qn, s), 0) < v:
+                queue[qn].wait_ge(T.sem[s], v)
+                known[(qn, s)] = v
+
+    def V(f, *args, w=()):
+        need("v", *w)
+        return done(f(*args), "kv")
+
+    def ts(out, i, a, b, o0, o1=None, w=()):
+        need("v", *w)
+        if o1 is None:
+            return done(vec.tensor_scalar(out, i, a, None, o0), "kv")
+        return done(vec.tensor_scalar(out, i, a, b, o0, o1), "kv")
+
+    tt, cp, ms, rd, scn, tr, qz = (vec.tensor_tensor, vec.tensor_copy, vec.memset, vec.tensor_reduce,
+                                   vec.tensor_tensor_scan, vec.transpose, vec.quantize_mx)
+
+    def load(qn, out, in_, sem):
+        return done(queue[qn].dma_start(out, in_), sem, 16)
+
+    dx = {}
+    dx[0] = load("y", T.xs[:, 0:512], T.x[:, 0:512], "dx0")
+    dp = load("s", T.pt[:, 0:128], T.p[:, 0:128], "dp")
+    dx[2] = load("s", T.xs[:, 1024:1536], T.x[:, 1024:1536], "dx2")
+    dx[1] = load("y", T.xs[:, 512:1024], T.x[:, 512:1024], "dx1")
+    dx[3] = load("s", T.xs[:, 1536:2048], T.x[:, 1536:2048], "dx3")
+
+    kpi = done(g.iota(T.pi[:], [[1, 1]], 0, 1), "kg")
+    done(g.iota(T.prmi[:], [[1, 8]], 0, 8), "kg")
+    done(g.iota(T.j4i[:], [[4, 32]], 0, 128), "kg")
+    kypi = done(g.iota(T.ypi[:], [[0, 32], [1, 4]], 0, 0), "kg")
+    kval = done(g.iota(T.val[:], [[4, 512]], 0, 0, allow_small_or_imprecise_dtypes=True), "kg")
+    V(ms, T.one2[:], 1.0)
+    V(ms, T.nn[:], 0.0)
+    V(ms, T.one[:], 1.0)
+    V(ms, T.k256[:], 256.0)
+    V(ms, T.z[:, 0:32], 0.0)
+    V(ms, T.iw[:], -1.0)
+    V(ms, T.gg[:], 0.0)
+    c = V(ms, T.reset[:], 0.0)
+    ts(T.pj[:, 0:1], T.pi[:], 31, None, A.bitwise_and, w=(kpi,))
+    ts(T.pj[:, 1:2], T.pi[:], 15, None, A.bitwise_and)
+    ts(T.pj[:, 2:3], T.pi[:], 3, None, A.bitwise_and)
+    c2 = ts(T.pj[:, 3:4], T.pi[:], 2, 3, A.logical_shift_right, A.bitwise_and)
+    V(ms, T.gg[:, 0:1], 99.0, w=(c,))
+    V(ms, T.reset[:, 0:256:16], -5e29)
+    c = V(cp, T.pf[:], T.pj[:], w=(c2,))
+    ts(T.c1[:], T.pf[:, 0:1], 0.0, 16.0, A.is_equal, A.mult, w=(c,))
+    ts(T.c3[:], T.pf[:, 0:1], 0.0, -273.0, A.is_equal, A.mult)
+    ts(T.c2[:], T.pf[:, 0:1], 15.0, None, A.is_equal)
+    ts(T.rst[:, 0:1], T.pf[:, 1:2], 4.0 * (r + 1) + 8192.0, -0.25, A.add, A.mult)
+    ts(T.rst[:, 1:2], T.pf[:, 1:2], 4.0 * (r + 1) + 8208.0, -0.25, A.add, A.mult)
+    tcol, rho = T.pf[:, 2:3], T.pf[:, 3:4]
+
+    c = V(cp, T.pt[:, 128:256], T.pt[:, 0:128], w=(dp,))
+    V(cp, T.pt[:, 512:576], T.pt[:, 0:64])
+    c = V(cp, T.pt[:, 256:512], T.pt[:, 0:256], w=(c,))
+    kqp = V(qz, T.qp[:], T.sp[:], T.pt[:], w=(c,))
+    c = ts(T.j4m[:], T.j4i[:], 4095, None, A.bitwise_and, w=(kypi,))
+    ts(T.prmi[:], T.prmi[:], 127, None, A.bitwise_and)
+    ts(T.msk[:], T.ypi[:], rho, None, A.is_equal)
+    ts(T.d0[:], T.ypi[:], 0.0, None, A.not_equal)
+    V(ms, T.ff[:, 0:160], 0.0)
+    V(cp, T.j4[:], T.j4m[:], w=(c,))
+    ts(T.trash[:], T.j4m[:], 0.25, 160.0, A.mult, A.add)
+    V(cp, T.prm[:], T.prmi[:], w=(("kv", cnt["kv"]),))
+
+    kqx = {}
+    for b in (0, 1):
+        k = 128 * b
+        o = T.ps[:, 512 * b:512 * b + 128]
+        for h in (0, 1):
+            i = b + 2 * h
+            kqx[i] = V(qz, T.qx[:, 128 * i:128 * i + 128], T.sx[:, 128 * i:128 * i + 128], T.xs[:, 512 * i:512 * i + 512],
+                       w=(dx[i],))
+            need("t", kqp, kqx[i])
+            m = done(ten.matmul_mx(o, T.qp[:, 16 * h:16 * h + 128], T.sp[:, 16 * h:16 * h + 128],
+                                   T.qx[:, 128 * i:128 * i + 128], T.sx[:, 128 * i:128 * i + 128], h == 0, h == 1), "kt")
+        c = V(tr, T.z[:, 32 + k:160 + k], o, w=(m,))
+        c = V(scn, T.mx[:, k:k + 128], T.z[:, 31 + k:159 + k], T.reset[:, k:k + 128], 0.0, A.max, A.add, w=(c,))
+        c = V(tt, T.nn[:, k:k + 128], T.z[:, 32 + k:160 + k], T.mx[:, k:k + 128], A.is_le, w=(c,))
+        c = V(scn, T.ss[:, k:k + 128], T.nn[:, k:k + 128], T.one2[:, k:k + 128], 0.0, A.mult, A.add, w=(c,))
+    for h in (0, 1):
+        src = T.ss[:, 16 * h + 15:256:32]
+        V(cp, T.gg[:, 1 + 8 * h:9 + 8 * h], src, w=(c,))
+        c2 = V(cp, T.gg[:, 32 + 8 * h:40 + 8 * h], src)
+    c = V(tr, T.h2[:], T.gg[:], w=(c2,))
+    here, prev = T.h2[:, 32:64], T.h2[:, 31:63]
+    kfl = V(tt, T.fl[:], here, prev, A.not_equal, w=(c,))
+    kz1 = ts(T.z1[:], T.h2[:, 32:33], T.c1[:], T.c3[:], A.mult, A.add)
+    V(scn, T.cs[:], T.one[:], T.fl[:], 0.0, A.mult, A.add, w=(kfl,))
+    kz2 = ts(T.z2[:], T.h2[:, 63:64], T.c2[:], T.z1[:], A.mult, A.add, w=(kz1,))
+    c = ts(T.dm[:], T.k256[:], T.cs[:, 31:32], T.z2[:], A.mult, A.add, w=(kz2,))
+    c = V(tr, T.dmt[:], T.dm[:], w=(c,))
+    c = V(rd, T.enc[:], T.dmt[:, 0:16], X, A.add, w=(c,))
+    ke16 = V(cp, T.e16[:, 0:1], T.enc[:], w=(c,))
+
+    arrive = {"e0": 0, "e1": 0}
+    for s in cores:
+        if s != core:
+            arrive["e0"] += len(_plan0(s, cores, topo).get(core, []))
+            arrive["e1"] += sum(len(es) for es in _plan(s, cores, topo)[core])
+    arrive["e2"] = arrive["e1"]
+
+    def did(d):
+        rid, pid, _ = topo.addr(d)
+        return DstId(rid=rid, pnc=pid)
+
+    groups = {}
+    for d, e in _plan0(core, cores, topo).items():
+        groups.setdefault(tuple(e), []).append(d)
+    if groups:
+        need("g", ke16)
+        g.remote_dma_fused(
+            [RemoteDMATransfer(dst_ids=[did(d) for d in ds], dma_engine_mask=_mask(e), remote_sem=T.sem.e0,
+                               srcs=[T.e16[:, 0:1]], dsts=[T.m16[:, r:r + 1] for d in ds]) for e, ds in groups.items()],
+            local_sem=T.sem.l0)
+        cnt["l0"] = sum(len(e) for e in groups)
+    need("y", ke16)
+    da = load("y", T.at[:], T.a[:], "da")
+    dw = load("y", T.wt[:], T.w[:], "dw")
+    dv = load("y", T.vt[:], T.v[:], "dv")
+
+    c = ts(T.dm2[:, 0:32], T.one[:], T.cs[:, 31:32], None, A.mult)
+    V(tt, T.nfe[:], here, prev, A.is_equal)
+    c2 = V(tt, T.fj[:], T.fl[:], T.j4[:], A.mult)
+    c = V(tr, T.dm2t[:, 0:32], T.dm2[:, 0:32], w=(c,))
+    V(rd, T.lj[:], T.fj[:], X, A.max, w=(c2,))
+    c = V(scn, T.iw[:, 1:17], T.one[:, 0:16], T.dm2t[:, 0:16], -1.0, A.mult, A.add, w=(c,))
+    for i in range(4):
+        V(tt, T.nfd[:, 16 * i:16 * i + 16], T.nfe[:, 16 * (i // 2):16 * (i // 2) + 16],
+          T.trash[:, 16 * (i // 2):16 * (i // 2) + 16], A.mult)
+    c = V(tr, T.ex[:], T.iw[:], w=(c,))
+    ts(T.dm2[:, 32:64], T.one[:], T.lj[:], None, A.mult)
+    for i in range(4):
+        c = ts(T.cd[:, 16 * i:16 * i + 16], T.cs[:, 16 * (i // 2):16 * (i // 2) + 16], T.ex[:, 0:1], None, A.add,
+               w=(c,) if i == 0 else ())
+    c = V(tt, T.od[:], T.cd[:], T.nfd[:], A.max, w=(c,))
+    c2 = V(tr, T.dm2t[:, 32:64], T.dm2[:, 32:64])
+    c = V(tr, T.to[:], T.od[:], w=(c,))
+    c2 = V(rd, T.last[:], T.dm2t[:, 32:48], X, A.max, w=(c2,))
+    V(cp, T.offl[:, 0:32:2], T.to[:, 0:16], w=(c,))
+    c = V(cp, T.offl[:, 1:32:2], T.to[:, 32:48])
+    klast = ts(T.lastl[:, 0:1], tcol, T.last[:], None, A.add, w=(c2,))
+    c = V(cp, T.ff[:, 0:FW].indirect(T.offl[:, 0:32]), T.val[:, 0:512], w=(c, kval))
+    if r:
+        V(cp, T.owni[:], T.enc[:])
+    c = V(tt, T.mk[:], T.ff[:, 0:128].indirect(T.prm[:, 0:8]), T.msk[:], A.mult, w=(c,))
+    if r:
+        ts(T.fi[:, r:r + 1], T.owni[:], 4, 15, A.logical_shift_right, A.bitwise_and, w=(c,))
+    c = V(scn, T.sg[:], T.d0[:], T.mk[:], 0.0, A.mult, A.add, w=(c,))
+    kuu = ts(T.uu[:], T.sg[:, 3:128:4], tcol, None, A.add, w=(c,))
+    for b in range(N):
+        need("s", klast, dx[0], dx[1], dx[2], dx[3])
+        klb = done(sca.activation(T.ct[:, 72 * b + 64:72 * b + 80], T.xs[:, 0:2048].indirect(T.lastl[:, 0:1]), AF.Copy), "ks")
+
+    if r == 0:
+        V(ms, T.bb[:], 0.0)
+        c = V(ms, T.nf0[:], 0.0)
+    else:
+        need("v", ("e0", arrive["e0"]))
+        cnt["e0"] = arrive["e0"]
+        c = V(cp, T.mi[:, 0:r], T.m16[:, 0:r])
+        if r > 1:
+            ts(T.fi[:, 1:r], T.mi[:, 1:r], 4, 15, A.logical_shift_right, A.bitwise_and, w=(c,))
+        c = ts(T.la[:, 0:r], T.mi[:, 0:r], 15, None, A.bitwise_and, w=(c,))
+        c2 = ts(T.ci[:, 0:r], T.mi[:, 0:r], 8, None, A.logical_shift_right)
+        c = V(tt, T.ne[:, 0:r], T.fi[:, 1:r + 1], T.la[:, 0:r], A.not_equal, w=(c,))
+        if r == 1:
+            c = V(tt, T.bb[:], T.ci[:, 0:1], T.ne[:, 0:1], A.add, w=(c,))
+        else:
+            c = V(tt, T.dd[:, 0:r], T.ci[:, 0:r], T.ne[:, 0:r], A.add, w=(c,))
+            c = V(rd, T.bb[:], T.dd[:, 0:r], X, A.add, w=(c,))
+    c = ts(T.ri[:], T.rst[:], T.bb[:], -4.0, A.add, A.mult, w=(("kv", cnt["kv"]),))
+    c = ts(T.ra[:], T.ri[:], 31, None, A.bitwise_and, w=(c,))
+    c = V(cp, T.ro[:], T.ra[:], w=(c,))
+    klst = V(cp, T.lst[:], T.uu[:, 0:32].indirect(T.ro[:, 0:2]), w=(c,))
+    for b in range(4, N):
+        need("s", klst, klb)
+        kcs2 = done(sca.activation(T.ct[:, 72 * b:72 * b + 64], T.xs[:, 0:2048].indirect(T.lst[:, 4 * b:4 * b + 4]), AF.Copy), "ks")
+    for b in range(0, 4):
+        c = V(cp, T.ct[:, 72 * b:72 * b + 64], T.xs[:, 0:2048].indirect(T.lst[:, 4 * b:4 * b + 4]), w=(klst, klb))
+    kqc = V(qz, T.qc[:, 0:NC], T.sc[:, 0:NC], T.ct[:, 0:4 * NC], w=(c, kcs2))
+
+    plan = _plan(core, cores, topo)
+
+    def exchange(codes, plane, first, rsem, lsem):
+        n = 0
+        for part in (0, 1):
+            tl = []
+            for d, es in plan.items():
+                k = first[d]
+                slot = NC + S * (((r - T.rank_of(d)) % N) - 1)
+                if part == 0:
+                    src, dst = codes[:, k:k + S].bitcast(dt.uint8), codes[:, slot:slot + S].bitcast(dt.uint8)
+                else:
+                    src, dst = plane[:, k:k + S], plane[:, slot:slot + S]
+                tl.append(RemoteDMATransfer(dst_ids=[did(d)], dma_engine_mask=_mask(es[part]), remote_sem=T.sem[rsem],
+                                            srcs=[src], dsts=[dst]))
+                n += len(es[part])
+            g.remote_dma_fused(tl, local_sem=T.sem[lsem])
+        cnt[lsem] = n
+
+    need("g", kqc)
+    exchange(T.qc, T.sc, {d: S * ((T.rank_of(d) - r - 1) % N) for d in plan}, "e1", "l1")
+
+    kqa = {}
+    for i in range(4):
+        kqa[i] = V(qz, T.qa[:, 128 * i:128 * i + 128], T.sa[:, 128 * i:128 * i + 128], T.at[:, 512 * i:512 * i + 512], w=(da,))
+    kqv = V(qz, T.qv[:], T.sv[:], T.vt[:], w=(dv,))
+    kqw = V(qz, T.qw[:], T.sw[:], T.wt[:], w=(dw,))
+    need("t", kqw, *kqx.values())
+    kwx = done(ten.matmul_mx(T.ps[:, 1024:1536], T.qw[:], T.sw[:], T.qx[:], T.sx[:], True, True), "kt")
+    need("s", kwx)
+    kwxs = done(sca.activation(T.wx[:], T.ps[:, 1024:1536], AF.Copy), "ks")
+    c = V(tr, T.tc[:], T.cd[:])
+    ts(T.lb0[:], here, -1.0, 16.0, A.mult, A.add)
+    ts(T.lb1[:, 0:16], T.cd[:, 0:16], T.bb[:], None, A.add)
+    klb1 = ts(T.lb1[:, 16:32], T.cd[:, 32:48], T.bb[:], None, A.add)
+    if r:
+        klb1 = V(tt, T.nf0[:], T.fi[:, r:r + 1], T.la[:, r - 1:r], A.is_equal)
+    ts(T.ii[:], T.tc[:], 0.125, -0.4375, A.mult, A.add, w=(c,))
+    c = ts(T.t1[:], T.tc[:], T.bb[:], float(N - r), A.add, A.add)
+    ts(T.fx[:], T.tc[:], 0.0, T.nf0[:], A.is_equal, A.mult, w=(klb1,))
+    c = ts(T.kk[:], T.t1[:], 7, None, A.bitwise_and, w=(c,))
+    c = ts(T.k18[:], T.kk[:], float(S), 1.0, A.mult, A.add, w=(c,))
+    c = V(tt, T.s1[:], T.k18[:], T.ii[:], A.add, w=(c,))
+    c = V(tt, T.s2[:], T.s1[:], T.fx[:], A.subtract, w=(c,))
+    V(cp, T.fin[:, 0:32:2], T.s2[:, 0:16], w=(c,))
+    kfin = V(cp, T.fin[:, 1:32:2], T.s2[:, 32:48])
+    need("y", klb1)
+    done(syn.dma_start(T.lb[0:1, :], T.lb0[0:16, :]), "dl0", 16)
+    done(syn.dma_start(T.lb[1:2, :], T.lb1[0:16, :]), "dl1", 16)
+
+    need("t", ("e1", arrive["e1"]), kqc)
+    cnt["e1"] = arrive["e1"]
+    kh = []
+    for i in range(4):
+        need("t", kqa[i])
+        o = T.ps[:, 2048 + 512 * i:2048 + 512 * i + NC]
+        m = done(ten.matmul_mx(o, T.qa[:, 128 * i:128 * i + 128], T.sa[:, 128 * i:128 * i + 128],
+                               T.qc[:, NC - S:NC + 126], T.sc[:, NC - S:NC + 126], True, True), "kt")
+        if i % 2:
+            need("s", m)
+            kh.append(done(sca.activation(T.ht[:, i:576:4], o, AF.Relu, 0.0, 0.05), "ks"))
+        else:
+            kh.append(ts(T.ht[:, i:576:4], o, 0.0, 0.05, A.max, A.mult, w=(m,)))
+    kqh = V(qz, T.qh[:, 0:NC], T.sh[:, 0:NC], T.ht[:], w=kh)
+    need("g", kqh)
+    exchange(T.qh, T.sh, {d: S * ((T.rank_of(d) - r) % N) - 1 for d in plan}, "e2", "l2")
+
+    need("t", kqh, kqv)
+    m = done(ten.matmul_mx(T.ps[:, 1536:1536 + NC], T.qv[:], T.sv[:], T.qh[:, 0:NC], T.sh[:, 0:NC], True, True), "kt")
+    V(cp, T.vw[:, 0:1], T.ps[:, 1536 + NC - 2:1536 + NC - 1], w=(m,))
+    V(cp, T.vw[:, 1:S], T.ps[:, 1536:1536 + S - 1])
+    need("t", ("e2", arrive["e2"]))
+    cnt["e2"] = arrive["e2"]
+    m = done(ten.matmul_mx(T.ps[:, 0:128], T.qv[:], T.sv[:], T.qh[:, NC - 2:NC + 126], T.sh[:, NC - 2:NC + 126], True, True), "kt")
+    c = V(cp, T.vw[:, S:NC], T.ps[:, 2:128], w=(m,))
+    for h in (0, 1):
+        k = 256 * h
+        c = V(tt, T.yt[:, k:k + 256], T.vw[:, 0:NC].indirect(T.fin[:, 16 * h:16 * h + 16]), T.wx[:, k:k + 256], A.add,
+              w=(c, kwxs, kfin) if h == 0 else ())
+        qn = "ys"[h]
+        need(qn, c)
+        done(queue[qn].dma_start(T.y[:, k:k + 256], T.yt[:, k:k + 256]), "dy%d" % h, 16)
+
+    for s in SEMAPHORES:
+        if cnt.get(s):
+            need("g", (s, cnt[s]))

@@ -5,6 +5,7 @@ N = 8
 S = 18
 NC = N * S
 FW = 160 + 512
+UW = 9 * 32
 
 F32, BF, I32, U16, C8, U8 = "float32", "bfloat16", "int32", "uint16", "float8_e4m3fn_x4", "uint8"
 
@@ -18,8 +19,8 @@ SCRATCH = {
     "xs": _sb(2048, BF), "pt": _sb(576, BF), "at": _sb(2048, BF), "wt": _sb(512, BF), "vt": _sb(512, BF),
     "qx": _sb(512, C8), "sx": _sb(512, U8), "qp": _sb(144, C8), "sp": _sb(144, U8),
     "qa": _sb(512, C8), "sa": _sb(512, U8), "qw": _sb(128, C8), "sw": _sb(128, U8), "qv": _sb(128, C8), "sv": _sb(128, U8),
-    "ct": _sb(592, BF), "qc": _sb(NC + 126, C8), "sc": _sb(NC + 126, U8),
-    "ht": _sb(576, BF), "qh": _sb(NC + 126, C8), "sh": _sb(NC + 126, U8),
+    "ct": _sb(592, BF), "qc": _sb(NC + 126, C8), "sc": _sb(NC + 126, U8), "lt": _sb(512, BF), "ql": _sb(128, C8),
+    "sl": _sb(128, U8), "ht": _sb(576, BF), "qh": _sb(NC + 126, C8), "sh": _sb(NC + 126, U8),
     "pi": _sb(1, I32), "pj": _sb(4, I32), "pf": _sb(4, F32), "j4i": _sb(32, I32), "j4m": _sb(32, I32), "j4": _sb(32, F32),
     "trash": _sb(32, F32), "val": _sb(512, F32), "prmi": _sb(8, I32), "prm": _sb(8, U16), "ypi": _sb(128, I32),
     "msk": _sb(128, F32), "d0": _sb(128, F32), "c1": _sb(1, F32), "c2": _sb(1, F32), "c3": _sb(1, F32), "rst": _sb(2, F32),
@@ -30,10 +31,10 @@ SCRATCH = {
     "fj": _sb(32, F32), "lj": _sb(1, F32), "dm2": _sb(64, F32), "dm2t": _sb(64, F32), "last": _sb(1, F32),
     "lastl": _sb(2, U16), "iw": _sb(32, F32), "ex": _sb(32, F32), "nfe": _sb(32, F32), "nfd": _sb(64, F32),
     "cd": _sb(64, F32), "od": _sb(64, F32), "to": _sb(64, F32), "offl": _sb(32, U16), "ff": _sb(FW, F32),
-    "mk": _sb(128, F32), "sg": _sb(128, F32), "uu": _sb(32, F32),
-    "m16": _sb(8, U16), "mi": _sb(8, I32), "fi": _sb(8, I32), "la": _sb(8, I32), "ci": _sb(8, I32), "ne": _sb(8, I32),
-    "dd": _sb(8, F32), "bb": _sb(1, F32), "nf0": _sb(1, F32), "ri": _sb(2, I32), "ra": _sb(2, I32), "ro": _sb(2, U16),
-    "lst": _sb(32, U16),
+    "mk": _sb(128, F32), "sg": _sb(128, F32), "uu": _sb(UW, F32),
+    "m16": _sb(8, U16), "mi": _sb(8, I32), "fi": _sb(8, I32), "la": _sb(8, I32), "c7": _sb(8, I32), "c7f": _sb(8, F32),
+    "ne": _sb(8, F32), "sb": _sb(8, F32), "ci": _sb(8, I32), "cif": _sb(8, F32), "sbb": _sb(8, F32), "nf0": _sb(1, F32),
+    "ro": _sb(2, U16), "lst": _sb(32, U16),
     "tc": _sb(64, F32), "ii": _sb(64, I32), "t1": _sb(64, I32), "kk": _sb(64, I32), "k18": _sb(64, F32), "fx": _sb(64, F32),
     "s1": _sb(64, F32), "s2": _sb(64, F32), "fin": _sb(32, U16), "lb0": _sb(32, F32), "lb1": _sb(32, F32),
     "wx": _sb(512, F32), "vw": _sb(NC, F32), "yt": _sb(512, F32),
@@ -71,6 +72,10 @@ def _plan0(core, cores, topo):
     return {d: eo if topo.chip(d) != ch else _near(core, d, eo, topo) for d in cores[cores.index(core) + 1:]}
 
 
+def _ahead(core, cores, topo):
+    return all(topo.chip(d) == topo.chip(core) for d in cores[cores.index(core) + 1:])
+
+
 def rank_program(g, core, T, topo):
     r = T.rank_of(core)
     if r is None:
@@ -102,6 +107,9 @@ def rank_program(g, core, T, topo):
             return done(vec.tensor_scalar(out, i, a, None, o0), "kv")
         return done(vec.tensor_scalar(out, i, a, b, o0, o1), "kv")
 
+    def io(out, pattern, base, cm):
+        return done(g.iota(out, pattern, base, cm, allow_small_or_imprecise_dtypes=True), "kg")
+
     tt, cp, ms, rd, scn, tr, qz = (vec.tensor_tensor, vec.tensor_copy, vec.memset, vec.tensor_reduce,
                                    vec.tensor_tensor_scan, vec.transpose, vec.quantize_mx)
 
@@ -115,61 +123,75 @@ def rank_program(g, core, T, topo):
     dx[1] = load("y", T.xs[:, 512:1024], T.x[:, 512:1024], "dx1")
     dx[3] = load("s", T.xs[:, 1536:2048], T.x[:, 1536:2048], "dx3")
 
-    kpi = done(g.iota(T.pi[:], [[1, 1]], 0, 1), "kg")
-    done(g.iota(T.prmi[:], [[1, 8]], 0, 8), "kg")
-    done(g.iota(T.j4i[:], [[4, 32]], 0, 128), "kg")
-    kypi = done(g.iota(T.ypi[:], [[0, 32], [1, 4]], 0, 0), "kg")
-    kval = done(g.iota(T.val[:], [[4, 512]], 0, 0, allow_small_or_imprecise_dtypes=True), "kg")
-    V(ms, T.one2[:], 1.0)
-    V(ms, T.nn[:], 0.0)
-    V(ms, T.one[:], 1.0)
-    V(ms, T.k256[:], 256.0)
-    V(ms, T.z[:, 0:32], 0.0)
-    V(ms, T.iw[:], -1.0)
-    V(ms, T.gg[:], 0.0)
+    ahead = _ahead(core, cores, topo)
+    kpi = io(T.pi[:], [[1, 1]], 0, 1)
+    io(T.prmi[:], [[1, 8]], 0, 8)
+    io(T.j4i[:], [[4, 32]], 0, 128)
+    kgg = io(T.gg[:], [[0, 64]], 0, 0)
+    kypi = io(T.ypi[:], [[0, 32], [1, 4]], 0, 0)
+    io(T.z[:, 0:32], [[0, 32]], 0, 0)
+    io(T.nn[:], [[0, 256]], 0, 0)
+    io(T.one2[:], [[0, 256]], 1, 0)
+    io(T.one[:], [[0, 32]], 1, 0)
+    kc = io(T.k256[:], [[0, 32]], 256, 0)
+    io(T.iw[:], [[0, 32]], -1, 0)
+    io(T.ff[:, 0:160], [[0, 160]], 0, 0)
+    kval = io(T.val[:], [[4, 512]], 0, 0)
+    if ahead:
+        kval = io(T.lt[:], [[0, 512]], 0, 0)
     c = V(ms, T.reset[:], 0.0)
     ts(T.pj[:, 0:1], T.pi[:], 31, None, A.bitwise_and, w=(kpi,))
     ts(T.pj[:, 1:2], T.pi[:], 15, None, A.bitwise_and)
     ts(T.pj[:, 2:3], T.pi[:], 3, None, A.bitwise_and)
     c2 = ts(T.pj[:, 3:4], T.pi[:], 2, 3, A.logical_shift_right, A.bitwise_and)
-    V(ms, T.gg[:, 0:1], 99.0, w=(c,))
-    V(ms, T.reset[:, 0:256:16], -5e29)
+    V(ms, T.reset[:, 0:256:16], -5e29, w=(c,))
     c = V(cp, T.pf[:], T.pj[:], w=(c2,))
+    V(ms, T.gg[:, 0:1], 99.0, w=(kgg,))
     ts(T.c1[:], T.pf[:, 0:1], 0.0, 16.0, A.is_equal, A.mult, w=(c,))
     ts(T.c3[:], T.pf[:, 0:1], 0.0, -273.0, A.is_equal, A.mult)
     ts(T.c2[:], T.pf[:, 0:1], 15.0, None, A.is_equal)
-    ts(T.rst[:, 0:1], T.pf[:, 1:2], 4.0 * (r + 1) + 8192.0, -0.25, A.add, A.mult)
-    ts(T.rst[:, 1:2], T.pf[:, 1:2], 4.0 * (r + 1) + 8208.0, -0.25, A.add, A.mult)
+    ts(T.rst[:, 0:1], T.pf[:, 1:2], 4.0 * (r + 1) + 224.0, -0.25, A.add, A.mult)
+    ts(T.rst[:, 1:2], T.pf[:, 1:2], 4.0 * (r + 1) + 240.0, -0.25, A.add, A.mult)
     tcol, rho = T.pf[:, 2:3], T.pf[:, 3:4]
+    c = ts(T.j4m[:], T.j4i[:], 4095, None, A.bitwise_and, w=(kypi,))
+    c2 = ts(T.prmi[:], T.prmi[:], 127, None, A.bitwise_and)
+    ts(T.msk[:], T.ypi[:], rho, None, A.is_equal)
+    ts(T.d0[:], T.ypi[:], 0.0, None, A.not_equal)
+    V(cp, T.j4[:], T.j4m[:], w=(c,))
+    ts(T.trash[:], T.j4m[:], 0.25, 160.0, A.mult, A.add)
+    V(cp, T.prm[:], T.prmi[:], w=(c2,))
 
     c = V(cp, T.pt[:, 128:256], T.pt[:, 0:128], w=(dp,))
     V(cp, T.pt[:, 512:576], T.pt[:, 0:64])
     c = V(cp, T.pt[:, 256:512], T.pt[:, 0:256], w=(c,))
     kqp = V(qz, T.qp[:], T.sp[:], T.pt[:], w=(c,))
-    c = ts(T.j4m[:], T.j4i[:], 4095, None, A.bitwise_and, w=(kypi,))
-    ts(T.prmi[:], T.prmi[:], 127, None, A.bitwise_and)
-    ts(T.msk[:], T.ypi[:], rho, None, A.is_equal)
-    ts(T.d0[:], T.ypi[:], 0.0, None, A.not_equal)
-    V(ms, T.ff[:, 0:160], 0.0)
-    V(cp, T.j4[:], T.j4m[:], w=(c,))
-    ts(T.trash[:], T.j4m[:], 0.25, 160.0, A.mult, A.add)
-    V(cp, T.prm[:], T.prmi[:], w=(("kv", cnt["kv"]),))
 
-    kqx = {}
-    for b in (0, 1):
-        k = 128 * b
-        o = T.ps[:, 512 * b:512 * b + 128]
-        for h in (0, 1):
-            i = b + 2 * h
-            kqx[i] = V(qz, T.qx[:, 128 * i:128 * i + 128], T.sx[:, 128 * i:128 * i + 128], T.xs[:, 512 * i:512 * i + 512],
-                       w=(dx[i],))
-            need("t", kqp, kqx[i])
-            m = done(ten.matmul_mx(o, T.qp[:, 16 * h:16 * h + 128], T.sp[:, 16 * h:16 * h + 128],
-                                   T.qx[:, 128 * i:128 * i + 128], T.sx[:, 128 * i:128 * i + 128], h == 0, h == 1), "kt")
-        c = V(tr, T.z[:, 32 + k:160 + k], o, w=(m,))
-        c = V(scn, T.mx[:, k:k + 128], T.z[:, 31 + k:159 + k], T.reset[:, k:k + 128], 0.0, A.max, A.add, w=(c,))
-        c = V(tt, T.nn[:, k:k + 128], T.z[:, 32 + k:160 + k], T.mx[:, k:k + 128], A.is_le, w=(c,))
-        c = V(scn, T.ss[:, k:k + 128], T.nn[:, k:k + 128], T.one2[:, k:k + 128], 0.0, A.mult, A.add, w=(c,))
+    kqx, ksc, kch = {}, {}, {}
+
+    def pack(i):
+        b, h = i % 2, i // 2
+        kqx[i] = V(qz, T.qx[:, 128 * i:128 * i + 128], T.sx[:, 128 * i:128 * i + 128], T.xs[:, 512 * i:512 * i + 512],
+                   w=(dx[i],))
+        need("t", kqp, kqx[i])
+        ksc[b] = done(ten.matmul_mx(T.ps[:, 512 * b:512 * b + 128], T.qp[:, 16 * h:16 * h + 128],
+                                    T.sp[:, 16 * h:16 * h + 128], T.qx[:, 128 * i:128 * i + 128],
+                                    T.sx[:, 128 * i:128 * i + 128], h == 0, h == 1), "kt")
+
+    def step(b, n):
+        k = slice(128 * b, 128 * b + 128)
+        z, before = T.z[:, 32 + 128 * b:160 + 128 * b], T.z[:, 31 + 128 * b:159 + 128 * b]
+        if n == 0:
+            kch[b] = V(tr, z, T.ps[:, 512 * b:512 * b + 128], w=(ksc[b],))
+        elif n == 1:
+            kch[b] = V(scn, T.mx[:, k], before, T.reset[:, k], 0.0, A.max, A.add, w=(kch[b], kc))
+        elif n == 2:
+            kch[b] = V(tt, T.nn[:, k], z, T.mx[:, k], A.is_le, w=(kch[b],))
+        else:
+            kch[b] = V(scn, T.ss[:, k], T.nn[:, k], T.one2[:, k], 0.0, A.mult, A.add, w=(kch[b],))
+        return kch[b]
+
+    pack(0), pack(2), step(0, 0), step(0, 1), pack(1), pack(3), step(0, 2), step(1, 0), step(0, 3), step(1, 1), step(1, 2)
+    c = step(1, 3)
     for h in (0, 1):
         src = T.ss[:, 16 * h + 15:256:32]
         V(cp, T.gg[:, 1 + 8 * h:9 + 8 * h], src, w=(c,))
@@ -185,12 +207,13 @@ def rank_program(g, core, T, topo):
     c = V(rd, T.enc[:], T.dmt[:, 0:16], X, A.add, w=(c,))
     ke16 = V(cp, T.e16[:, 0:1], T.enc[:], w=(c,))
 
-    arrive = {"e0": 0, "e1": 0}
+    arrive = {"e0": 0, "e1": 0, "e2": 0}
     for s in cores:
         if s != core:
+            n = sum(len(es) for es in _plan(s, cores, topo)[core])
             arrive["e0"] += len(_plan0(s, cores, topo).get(core, []))
-            arrive["e1"] += sum(len(es) for es in _plan(s, cores, topo)[core])
-    arrive["e2"] = arrive["e1"]
+            arrive["e1"] += n * (2 if _ahead(s, cores, topo) else 1)
+            arrive["e2"] += n
 
     def did(d):
         rid, pid, _ = topo.addr(d)
@@ -211,12 +234,30 @@ def rank_program(g, core, T, topo):
     dw = load("y", T.wt[:], T.w[:], "dw")
     dv = load("y", T.vt[:], T.v[:], "dv")
 
+    plan = _plan(core, cores, topo)
+
+    def exchange(codes, plane, first, width, at, rsem, lsem):
+        land = (T.qc, T.sc) if rsem == "e1" else (T.qh, T.sh)
+        for part in (0, 1):
+            tl = []
+            for d, es in plan.items():
+                k = first[d]
+                slot = NC + S * (((r - T.rank_of(d)) % N) - 1) + at
+                if part == 0:
+                    src, dst = codes[:, k:k + width].bitcast(dt.uint8), land[0][:, slot:slot + width].bitcast(dt.uint8)
+                else:
+                    src, dst = plane[:, k:k + width], land[1][:, slot:slot + width]
+                tl.append(RemoteDMATransfer(dst_ids=[did(d)], dma_engine_mask=_mask(es[part]), remote_sem=T.sem[rsem],
+                                            srcs=[src], dsts=[dst]))
+                cnt[lsem] = cnt.get(lsem, 0) + len(es[part])
+            g.remote_dma_fused(tl, local_sem=T.sem[lsem])
+
     c = ts(T.dm2[:, 0:32], T.one[:], T.cs[:, 31:32], None, A.mult)
     V(tt, T.nfe[:], here, prev, A.is_equal)
     c2 = V(tt, T.fj[:], T.fl[:], T.j4[:], A.mult)
     c = V(tr, T.dm2t[:, 0:32], T.dm2[:, 0:32], w=(c,))
     V(rd, T.lj[:], T.fj[:], X, A.max, w=(c2,))
-    c = V(scn, T.iw[:, 1:17], T.one[:, 0:16], T.dm2t[:, 0:16], -1.0, A.mult, A.add, w=(c,))
+    c = V(scn, T.iw[:, 1:17], T.one[:, 0:16], T.dm2t[:, 0:16], -1.0, A.mult, A.add, w=(c, kval))
     for i in range(4):
         V(tt, T.nfd[:, 16 * i:16 * i + 16], T.nfe[:, 16 * (i // 2):16 * (i // 2) + 16],
           T.trash[:, 16 * (i // 2):16 * (i // 2) + 16], A.mult)
@@ -229,70 +270,56 @@ def rank_program(g, core, T, topo):
     c2 = V(tr, T.dm2t[:, 32:64], T.dm2[:, 32:64])
     c = V(tr, T.to[:], T.od[:], w=(c,))
     c2 = V(rd, T.last[:], T.dm2t[:, 32:48], X, A.max, w=(c2,))
+    klast = ts(T.lastl[:, 0:1], tcol, T.last[:], None, A.add, w=(c2,))
     V(cp, T.offl[:, 0:32:2], T.to[:, 0:16], w=(c,))
     c = V(cp, T.offl[:, 1:32:2], T.to[:, 32:48])
-    klast = ts(T.lastl[:, 0:1], tcol, T.last[:], None, A.add, w=(c2,))
-    c = V(cp, T.ff[:, 0:FW].indirect(T.offl[:, 0:32]), T.val[:, 0:512], w=(c, kval))
+    need("s", klast, kval, dx[0], dx[1], dx[2], dx[3])
+    if ahead:
+        klt = done(sca.activation(T.lt[:, 0:16], T.xs[:, 0:2048].indirect(T.lastl[:, 0:1]), AF.Copy), "ks")
+        klt = V(qz, T.ql[:], T.sl[:], T.lt[:], w=(klt,))
+        need("g", klt)
+        exchange(T.ql, T.sl, {d: 0 for d in plan}, 2, 16, "e1", "l1")
+    for b in range(N):
+        klb = done(sca.activation(T.ct[:, 72 * b + 64:72 * b + 80], T.xs[:, 0:2048].indirect(T.lastl[:, 0:1]), AF.Copy), "ks")
+    c = V(cp, T.ff[:, 0:FW].indirect(T.offl[:, 0:32]), T.val[:, 0:512], w=(c,))
     if r:
         V(cp, T.owni[:], T.enc[:])
     c = V(tt, T.mk[:], T.ff[:, 0:128].indirect(T.prm[:, 0:8]), T.msk[:], A.mult, w=(c,))
     if r:
         ts(T.fi[:, r:r + 1], T.owni[:], 4, 15, A.logical_shift_right, A.bitwise_and, w=(c,))
     c = V(scn, T.sg[:], T.d0[:], T.mk[:], 0.0, A.mult, A.add, w=(c,))
-    kuu = ts(T.uu[:], T.sg[:, 3:128:4], tcol, None, A.add, w=(c,))
-    for b in range(N):
-        need("s", klast, dx[0], dx[1], dx[2], dx[3])
-        klb = done(sca.activation(T.ct[:, 72 * b + 64:72 * b + 80], T.xs[:, 0:2048].indirect(T.lastl[:, 0:1]), AF.Copy), "ks")
+    c = ts(T.uu[:, 0:32], T.sg[:, 3:128:4], tcol, None, A.add, w=(c,))
+    c = V(cp, T.uu[:, 32:64], T.uu[:, 0:32], w=(c,))
+    c = V(cp, T.uu[:, 64:128], T.uu[:, 0:64], w=(c,))
+    V(cp, T.uu[:, 128:256], T.uu[:, 0:128], w=(c,))
+    kuu = V(cp, T.uu[:, 256:288], T.uu[:, 0:32])
 
     if r == 0:
-        V(ms, T.bb[:], 0.0)
-        c = V(ms, T.nf0[:], 0.0)
+        V(ms, T.nf0[:], 0.0)
+        sb = sbb = T.sb[:, 0:1]
+        c = V(ms, sb, 0.0)
     else:
         need("v", ("e0", arrive["e0"]))
         cnt["e0"] = arrive["e0"]
+        sb, sbb = T.sb[:, r - 1:r], T.sbb[:, r - 1:r]
         c = V(cp, T.mi[:, 0:r], T.m16[:, 0:r])
         if r > 1:
             ts(T.fi[:, 1:r], T.mi[:, 1:r], 4, 15, A.logical_shift_right, A.bitwise_and, w=(c,))
         c = ts(T.la[:, 0:r], T.mi[:, 0:r], 15, None, A.bitwise_and, w=(c,))
-        c2 = ts(T.ci[:, 0:r], T.mi[:, 0:r], 8, None, A.logical_shift_right)
-        c = V(tt, T.ne[:, 0:r], T.fi[:, 1:r + 1], T.la[:, 0:r], A.not_equal, w=(c,))
-        if r == 1:
-            c = V(tt, T.bb[:], T.ci[:, 0:1], T.ne[:, 0:1], A.add, w=(c,))
-        else:
-            c = V(tt, T.dd[:, 0:r], T.ci[:, 0:r], T.ne[:, 0:r], A.add, w=(c,))
-            c = V(rd, T.bb[:], T.dd[:, 0:r], X, A.add, w=(c,))
-    c = ts(T.ri[:], T.rst[:], T.bb[:], -4.0, A.add, A.mult, w=(("kv", cnt["kv"]),))
-    c = ts(T.ra[:], T.ri[:], 31, None, A.bitwise_and, w=(c,))
-    c = V(cp, T.ro[:], T.ra[:], w=(c,))
-    klst = V(cp, T.lst[:], T.uu[:, 0:32].indirect(T.ro[:, 0:2]), w=(c,))
+        c2 = ts(T.c7[:, 0:r], T.mi[:, 0:r], 8, 7, A.logical_shift_right, A.bitwise_and)
+        V(tt, T.ne[:, 0:r], T.fi[:, 1:r + 1], T.la[:, 0:r], A.not_equal, w=(c,))
+        c = V(cp, T.c7f[:, 0:r], T.c7[:, 0:r], w=(c2,))
+        c = V(scn, T.sb[:, 0:r], T.c7f[:, 0:r], T.ne[:, 0:r], 0.0, A.add, A.add, w=(c,))
+    c = ts(T.ro[:], T.rst[:], sb, -4.0, A.add, A.mult, w=(c, kuu))
+    klst = V(cp, T.lst[:], T.uu[:, 0:UW].indirect(T.ro[:, 0:2]), w=(c,))
+    need("s", klst, klb)
     for b in range(4, N):
-        need("s", klst, klb)
         kcs2 = done(sca.activation(T.ct[:, 72 * b:72 * b + 64], T.xs[:, 0:2048].indirect(T.lst[:, 4 * b:4 * b + 4]), AF.Copy), "ks")
     for b in range(0, 4):
         c = V(cp, T.ct[:, 72 * b:72 * b + 64], T.xs[:, 0:2048].indirect(T.lst[:, 4 * b:4 * b + 4]), w=(klst, klb))
     kqc = V(qz, T.qc[:, 0:NC], T.sc[:, 0:NC], T.ct[:, 0:4 * NC], w=(c, kcs2))
-
-    plan = _plan(core, cores, topo)
-
-    def exchange(codes, plane, first, rsem, lsem):
-        n = 0
-        for part in (0, 1):
-            tl = []
-            for d, es in plan.items():
-                k = first[d]
-                slot = NC + S * (((r - T.rank_of(d)) % N) - 1)
-                if part == 0:
-                    src, dst = codes[:, k:k + S].bitcast(dt.uint8), codes[:, slot:slot + S].bitcast(dt.uint8)
-                else:
-                    src, dst = plane[:, k:k + S], plane[:, slot:slot + S]
-                tl.append(RemoteDMATransfer(dst_ids=[did(d)], dma_engine_mask=_mask(es[part]), remote_sem=T.sem[rsem],
-                                            srcs=[src], dsts=[dst]))
-                n += len(es[part])
-            g.remote_dma_fused(tl, local_sem=T.sem[lsem])
-        cnt[lsem] = n
-
     need("g", kqc)
-    exchange(T.qc, T.sc, {d: S * ((T.rank_of(d) - r - 1) % N) for d in plan}, "e1", "l1")
+    exchange(T.qc, T.sc, {d: S * ((T.rank_of(d) - r - 1) % N) for d in plan}, 16 if ahead else S, 0, "e1", "l1")
 
     kqa = {}
     for i in range(4):
@@ -303,16 +330,19 @@ def rank_program(g, core, T, topo):
     kwx = done(ten.matmul_mx(T.ps[:, 1024:1536], T.qw[:], T.sw[:], T.qx[:], T.sx[:], True, True), "kt")
     need("s", kwx)
     kwxs = done(sca.activation(T.wx[:], T.ps[:, 1024:1536], AF.Copy), "ks")
-    c = V(tr, T.tc[:], T.cd[:])
-    ts(T.lb0[:], here, -1.0, 16.0, A.mult, A.add)
-    ts(T.lb1[:, 0:16], T.cd[:, 0:16], T.bb[:], None, A.add)
-    klb1 = ts(T.lb1[:, 16:32], T.cd[:, 32:48], T.bb[:], None, A.add)
     if r:
-        klb1 = V(tt, T.nf0[:], T.fi[:, r:r + 1], T.la[:, r - 1:r], A.is_equal)
+        c = ts(T.ci[:, 0:r], T.mi[:, 0:r], 8, None, A.logical_shift_right)
+        V(tt, T.nf0[:], T.fi[:, r:r + 1], T.la[:, r - 1:r], A.is_equal)
+        c = V(cp, T.cif[:, 0:r], T.ci[:, 0:r], w=(c,))
+        V(scn, T.sbb[:, 0:r], T.cif[:, 0:r], T.ne[:, 0:r], 0.0, A.add, A.add, w=(c,))
+    ts(T.lb0[:], here, -1.0, 16.0, A.mult, A.add)
+    c = V(tr, T.tc[:], T.cd[:])
     ts(T.ii[:], T.tc[:], 0.125, -0.4375, A.mult, A.add, w=(c,))
-    c = ts(T.t1[:], T.tc[:], T.bb[:], float(N - r), A.add, A.add)
-    ts(T.fx[:], T.tc[:], 0.0, T.nf0[:], A.is_equal, A.mult, w=(klb1,))
+    c = ts(T.t1[:], T.tc[:], sb, float(N - r), A.add, A.add)
+    ts(T.fx[:], T.tc[:], 0.0, T.nf0[:], A.is_equal, A.mult)
     c = ts(T.kk[:], T.t1[:], 7, None, A.bitwise_and, w=(c,))
+    ts(T.lb1[:, 0:16], T.cd[:, 0:16], sbb, None, A.add)
+    klb1 = ts(T.lb1[:, 16:32], T.cd[:, 32:48], sbb, None, A.add)
     c = ts(T.k18[:], T.kk[:], float(S), 1.0, A.mult, A.add, w=(c,))
     c = V(tt, T.s1[:], T.k18[:], T.ii[:], A.add, w=(c,))
     c = V(tt, T.s2[:], T.s1[:], T.fx[:], A.subtract, w=(c,))
@@ -337,7 +367,7 @@ def rank_program(g, core, T, topo):
             kh.append(ts(T.ht[:, i:576:4], o, 0.0, 0.05, A.max, A.mult, w=(m,)))
     kqh = V(qz, T.qh[:, 0:NC], T.sh[:, 0:NC], T.ht[:], w=kh)
     need("g", kqh)
-    exchange(T.qh, T.sh, {d: S * ((T.rank_of(d) - r) % N) - 1 for d in plan}, "e2", "l2")
+    exchange(T.qh, T.sh, {d: S * ((T.rank_of(d) - r) % N) - 1 for d in plan}, S, 0, "e2", "l2")
 
     need("t", kqh, kqv)
     m = done(ten.matmul_mx(T.ps[:, 1536:1536 + NC], T.qv[:], T.sv[:], T.qh[:, 0:NC], T.sh[:, 0:NC], True, True), "kt")

@@ -4,8 +4,9 @@ from concourse.mybir import dt, AluOpType, AxisListType, ActivationFunctionType
 N = 8
 S = 18
 NC = N * S
-FW = 160 + 512
-UW = 9 * 32
+ROOM = 160
+FW = ROOM + 512 + 128
+UW = N * 32
 
 F32, BF, I32, U16, C8, U8 = "float32", "bfloat16", "int32", "uint16", "float8_e4m3fn_x4", "uint8"
 
@@ -22,25 +23,27 @@ SCRATCH = {
     "ct": _sb(592, BF), "qc": _sb(NC + 126, C8), "sc": _sb(NC + 126, U8), "lt": _sb(512, BF), "ql": _sb(128, C8),
     "sl": _sb(128, U8), "ht": _sb(576, BF), "qh": _sb(NC + 126, C8), "sh": _sb(NC + 126, U8),
     "pi": _sb(1, I32), "pj": _sb(4, I32), "pf": _sb(4, F32), "j4i": _sb(32, I32), "j4m": _sb(32, I32), "j4": _sb(32, F32),
-    "trash": _sb(32, F32), "val": _sb(512, F32), "prmi": _sb(8, I32), "prm": _sb(8, U16), "ypi": _sb(128, I32),
-    "msk": _sb(128, F32), "d0": _sb(128, F32), "c1": _sb(1, F32), "c2": _sb(1, F32), "c3": _sb(1, F32), "rst": _sb(2, F32),
-    "reset": _sb(256, F32), "one2": _sb(256, BF), "one": _sb(32, F32), "k256": _sb(32, F32),
+    "trash": _sb(32, F32), "vali": _sb(256, F32), "val": _sb(256, F32), "prmi": _sb(8, I32), "prm": _sb(8, U16),
+    "ypi": _sb(128, I32), "msk": _sb(128, F32), "d0": _sb(128, F32), "c0": _sb(1, F32), "c1": _sb(1, F32),
+    "c2": _sb(1, F32), "c3": _sb(1, F32), "kr": _sb(1, F32), "th": _sb(1, F32), "lane": _sb(1, F32), "g64": _sb(1, F32),
+    "rst": _sb(2, F32), "reset": _sb(128, F32), "one2": _sb(128, BF), "one": _sb(32, F32), "kw": _sb(32, F32),
     "z": _sb(288, F32), "mx": _sb(256, F32), "nn": _sb(256, BF), "ss": _sb(256, BF), "gg": _sb(64, F32), "h2": _sb(64, F32),
-    "fl": _sb(32, F32), "cs": _sb(32, F32), "z1": _sb(1, F32), "z2": _sb(1, F32), "dm": _sb(32, F32), "dmt": _sb(32, F32),
-    "enc": _sb(1, F32), "e16": _sb(2, U16), "owni": _sb(1, I32),
-    "fj": _sb(32, F32), "lj": _sb(1, F32), "dm2": _sb(64, F32), "dm2t": _sb(64, F32), "last": _sb(1, F32),
-    "lastl": _sb(2, U16), "iw": _sb(32, F32), "ex": _sb(32, F32), "nfe": _sb(32, F32), "nfd": _sb(64, F32),
-    "cd": _sb(64, F32), "od": _sb(64, F32), "to": _sb(64, F32), "offl": _sb(32, U16), "ff": _sb(FW, F32),
-    "mk": _sb(128, F32), "sg": _sb(128, F32), "uu": _sb(UW, F32),
+    "fl": _sb(32, F32), "cc": _sb(64, F32), "cct": _sb(64, F32), "z1": _sb(1, F32), "z2": _sb(1, F32), "dm": _sb(32, F32),
+    "dmt": _sb(32, F32), "enc": _sb(1, F32), "e16": _sb(2, U16), "owni": _sb(1, I32),
+    "fj": _sb(32, F32), "lj": _sb(1, F32), "dm2": _sb(32, F32), "dm2t": _sb(32, F32), "last": _sb(1, F32),
+    "lastl": _sb(2, U16), "iw": _sb(32, F32), "nfe": _sb(32, F32), "nfd": _sb(32, F32),
+    "offf": _sb(16, F32), "offl": _sb(16, U16), "ff": _sb(FW, F32),
+    "mk": _sb(128, F32), "sg": _sb(128, F32), "u0": _sb(32, F32), "ut": _sb(32, F32), "us": _sb(32, F32), "uu": _sb(UW, F32),
     "m16": _sb(8, U16), "mi": _sb(8, I32), "fi": _sb(8, I32), "la": _sb(8, I32), "c7": _sb(8, I32), "c7f": _sb(8, F32),
     "ne": _sb(8, F32), "sb": _sb(8, F32), "ci": _sb(8, I32), "cif": _sb(8, F32), "sbb": _sb(8, F32), "nf0": _sb(1, F32),
     "ro": _sb(2, U16), "lst": _sb(32, U16),
+    "tcs": _sb(32, F32), "cdw": _sb(32, F32), "cd": _sb(64, F32),
     "tc": _sb(64, F32), "ii": _sb(64, I32), "t1": _sb(64, I32), "kk": _sb(64, I32), "k18": _sb(64, F32), "fx": _sb(64, F32),
     "s1": _sb(64, F32), "s2": _sb(64, F32), "fin": _sb(32, U16), "lb0": _sb(32, F32), "lb1": _sb(32, F32),
     "wx": _sb(512, F32), "vw": _sb(NC, F32), "yt": _sb(512, F32),
 }
-SEMAPHORES = ["kv", "ks", "kt", "kg", "dp", "dx0", "dx1", "dx2", "dx3", "da", "dw", "dv", "dy0", "dy1", "dl0", "dl1",
-              "e0", "e1", "e2", "l0", "l1", "l2"]
+SEMAPHORES = ["kv", "ks", "kt", "kg", "dp", "dx0", "dx1", "dx2", "dx3", "da0", "da1", "dw", "dv", "dy0", "dy1", "dy2",
+              "dl0", "dl1", "e0", "e1", "e2", "l0", "l1", "l2"]
 
 
 def _mask(es):
@@ -58,8 +61,8 @@ def _plan(core, cores, topo):
     eo = topo.engines(core, off[0])
     plan = {}
     for i, d in enumerate(off):
-        j = 2 * (i - 4)
-        plan[d] = ([eo[i]], [eo[4 + i]]) if i < 4 else (eo[4 + j:6 + j], eo[j:j + 2])
+        j = 4 * (i - 4)
+        plan[d] = ([eo[2 * i]], [eo[2 * i + 1]]) if i < 4 else (eo[j + 1:j + 4:2], eo[j:j + 4:2])
     for d in cores:
         if d != core and topo.chip(d) == ch:
             plan[d] = (_near(core, d, eo, topo),) * 2
@@ -110,6 +113,14 @@ def rank_program(g, core, T, topo):
     def io(out, pattern, base, cm):
         return done(g.iota(out, pattern, base, cm, allow_small_or_imprecise_dtypes=True), "kg")
 
+    def sc(out, in_, w=()):
+        need("s", *w)
+        return done(sca.activation(out, in_, AF.Copy), "ks")
+
+    def si(out, in_, bias, scale, w=()):
+        need("s", *w)
+        return done(sca.activation(out, in_, AF.Identity, bias, scale), "ks")
+
     tt, cp, ms, rd, scn, tr, qz = (vec.tensor_tensor, vec.tensor_copy, vec.memset, vec.tensor_reduce,
                                    vec.tensor_tensor_scan, vec.transpose, vec.quantize_mx)
 
@@ -122,44 +133,56 @@ def rank_program(g, core, T, topo):
     dx[2] = load("s", T.xs[:, 1024:1536], T.x[:, 1024:1536], "dx2")
     dx[1] = load("y", T.xs[:, 512:1024], T.x[:, 512:1024], "dx1")
     dx[3] = load("s", T.xs[:, 1536:2048], T.x[:, 1536:2048], "dx3")
-
+    da = [load("s", T.at[:, 0:1024], T.a[:, 0:1024], "da0")]
     ahead = _ahead(core, cores, topo)
-    kpi = io(T.pi[:], [[1, 1]], 0, 1)
-    io(T.prmi[:], [[1, 8]], 0, 8)
-    io(T.j4i[:], [[4, 32]], 0, 128)
-    kgg = io(T.gg[:], [[0, 64]], 0, 0)
-    kypi = io(T.ypi[:], [[0, 32], [1, 4]], 0, 0)
-    io(T.z[:, 0:32], [[0, 32]], 0, 0)
-    io(T.nn[:], [[0, 256]], 0, 0)
-    io(T.one2[:], [[0, 256]], 1, 0)
-    io(T.one[:], [[0, 32]], 1, 0)
-    kc = io(T.k256[:], [[0, 32]], 256, 0)
-    io(T.iw[:], [[0, 32]], -1, 0)
-    io(T.ff[:, 0:160], [[0, 160]], 0, 0)
-    kval = io(T.val[:], [[4, 512]], 0, 0)
     if ahead:
-        kval = io(T.lt[:], [[0, 512]], 0, 0)
+        da.append(load("s", T.at[:, 1024:2048], T.a[:, 1024:2048], "da1"))
+        dv = load("s", T.vt[:], T.v[:], "dv")
+        dw = load("s", T.wt[:], T.w[:], "dw")
+
+    kpi = io(T.pi[:], [[1, 1]], 0, 1)
+    kj4 = io(T.j4i[:], [[4, 32]], 0, 128)
+    kone = io(T.one[:], [[0, 32]], 1, 0)
+    kypi = io(T.ypi[:], [[0, 32], [1, 4]], 0, 0)
+    kprm = io(T.prmi[:], [[1, 8]], 0, 8)
+    kgg = io(T.gg[:], [[0, 64]], 0, 0)
+    io(T.z[:, 24:32], [[0, 8]], 0, 0)
+    kc = io(T.one2[:], [[0, 128]], 1, 0)
+    kval = io(T.vali[:], [[128, 16], [4, 16]], 0, 0)
+    io(T.iw[:], [[0, 32]], 0, 0)
+    kff = io(T.ff[:, 0:ROOM], [[0, ROOM]], 0, 0)
+    if ahead:
+        kff = io(T.lt[:], [[0, 512]], 0, 0)
     c = V(ms, T.reset[:], 0.0)
     ts(T.pj[:, 0:1], T.pi[:], 31, None, A.bitwise_and, w=(kpi,))
     ts(T.pj[:, 1:2], T.pi[:], 15, None, A.bitwise_and)
     ts(T.pj[:, 2:3], T.pi[:], 3, None, A.bitwise_and)
     c2 = ts(T.pj[:, 3:4], T.pi[:], 2, 3, A.logical_shift_right, A.bitwise_and)
-    V(ms, T.reset[:, 0:256:16], -5e29, w=(c,))
-    c = V(cp, T.pf[:], T.pj[:], w=(c2,))
-    V(ms, T.gg[:, 0:1], 99.0, w=(kgg,))
-    ts(T.c1[:], T.pf[:, 0:1], 0.0, 16.0, A.is_equal, A.mult, w=(c,))
-    ts(T.c3[:], T.pf[:, 0:1], 0.0, -273.0, A.is_equal, A.mult)
-    ts(T.c2[:], T.pf[:, 0:1], 15.0, None, A.is_equal)
-    ts(T.rst[:, 0:1], T.pf[:, 1:2], 4.0 * (r + 1) + 224.0, -0.25, A.add, A.mult)
-    ts(T.rst[:, 1:2], T.pf[:, 1:2], 4.0 * (r + 1) + 240.0, -0.25, A.add, A.mult)
+    V(ms, T.reset[:, 0:128:16], -5e29, w=(c,))
+    cpf = V(cp, T.pf[:], T.pj[:], w=(c2,))
+    c = ts(T.j4m[:], T.j4i[:], 4095, None, A.bitwise_and, w=(kj4,))
+    ckr = ts(T.kr[:], T.pf[:, 0:1], 16.0, None, A.is_lt, w=(cpf,))
+    cg = V(tt, T.lane[:], T.pf[:, 0:1], T.pf[:, 1:2], A.subtract)
+    cj4 = V(cp, T.j4[:], T.j4m[:], w=(c,))
+    ts(T.c0[:], T.pf[:, 0:1], 0.0, -1.0, A.is_equal, A.mult)
+    ts(T.c1[:], T.pf[:, 0:1], 17.0, 16.0 / 256, A.is_equal, A.mult)
+    ts(T.c3[:], T.pf[:, 0:1], 17.0, -17.0 / 256, A.is_equal, A.mult)
+    ts(T.c2[:], T.pf[:, 0:1], 16.0, 1.0 / 256, A.is_equal, A.mult)
     tcol, rho = T.pf[:, 2:3], T.pf[:, 3:4]
-    c = ts(T.j4m[:], T.j4i[:], 4095, None, A.bitwise_and, w=(kypi,))
-    c2 = ts(T.prmi[:], T.prmi[:], 127, None, A.bitwise_and)
-    ts(T.msk[:], T.ypi[:], rho, None, A.is_equal)
+    ts(T.msk[:], T.ypi[:], rho, None, A.is_equal, w=(kypi,))
     ts(T.d0[:], T.ypi[:], 0.0, None, A.not_equal)
-    V(cp, T.j4[:], T.j4m[:], w=(c,))
-    ts(T.trash[:], T.j4m[:], 0.25, 160.0, A.mult, A.add)
+    c2 = ts(T.prmi[:], T.prmi[:], 127, None, A.bitwise_and, w=(kprm,))
+    V(ms, T.gg[:, 0:1], 99.0, w=(kgg,))
     V(cp, T.prm[:], T.prmi[:], w=(c2,))
+    turn = 4.0 * ((r + 1) % N) + 4.0 * N * r
+    si(T.th[:], T.pf[:, 2:3], 0.0, 0.5, w=(cpf,))
+    si(T.rst[:, 0:1], T.pf[:, 1:2], -0.25 * turn, -0.25)
+    si(T.rst[:, 1:2], T.pf[:, 1:2], -0.25 * (turn + 16.0), -0.25)
+    need("s", kone, ckr)
+    si(T.kw[:], T.one[:], 0.0, T.kr[:])
+    kg64 = si(T.g64[:], T.lane[:], 0.0, 4.0, w=(cg,))
+    si(T.trash[:], T.j4[:], float(ROOM), 0.25, w=(cj4,))
+    kval = si(T.val[:], T.vali[:], T.g64[:], 1.0, w=(kval, kg64))
 
     c = V(cp, T.pt[:, 128:256], T.pt[:, 0:128], w=(dp,))
     V(cp, T.pt[:, 512:576], T.pt[:, 0:64])
@@ -183,29 +206,35 @@ def rank_program(g, core, T, topo):
         if n == 0:
             kch[b] = V(tr, z, T.ps[:, 512 * b:512 * b + 128], w=(ksc[b],))
         elif n == 1:
-            kch[b] = V(scn, T.mx[:, k], before, T.reset[:, k], 0.0, A.max, A.add, w=(kch[b], kc))
+            kch[b] = V(scn, T.mx[:, k], before, T.reset[:], 0.0, A.max, A.add, w=(kch[b], kc))
         elif n == 2:
             kch[b] = V(tt, T.nn[:, k], z, T.mx[:, k], A.is_le, w=(kch[b],))
         else:
-            kch[b] = V(scn, T.ss[:, k], T.nn[:, k], T.one2[:, k], 0.0, A.mult, A.add, w=(kch[b],))
+            kch[b] = V(scn, T.ss[:, k], T.nn[:, k], T.one2[:], 0.0, A.mult, A.add, w=(kch[b],))
         return kch[b]
 
-    pack(0), pack(2), step(0, 0), step(0, 1), pack(1), pack(3), step(0, 2), step(1, 0), step(0, 3), step(1, 1), step(1, 2)
+    pack(0), pack(2), step(0, 0), step(0, 1), pack(1), pack(3), step(0, 2), step(1, 0), step(0, 3), step(1, 1)
+    V(cp, T.gg[:, 17:18], T.ss[:, 15:16], w=(kch[0],))
+    step(1, 2)
     c = step(1, 3)
     for h in (0, 1):
-        src = T.ss[:, 16 * h + 15:256:32]
-        V(cp, T.gg[:, 1 + 8 * h:9 + 8 * h], src, w=(c,))
-        c2 = V(cp, T.gg[:, 32 + 8 * h:40 + 8 * h], src)
+        V(cp, T.gg[:, 1 + 8 * h:9 + 8 * h], T.ss[:, 16 * h + 15:256:32], w=(c,))
+        c2 = V(cp, T.gg[:, 32 + 8 * h:40 + 8 * h], T.ss[:, 16 * h + 15:256:32])
     c = V(tr, T.h2[:], T.gg[:], w=(c2,))
     here, prev = T.h2[:, 32:64], T.h2[:, 31:63]
     kfl = V(tt, T.fl[:], here, prev, A.not_equal, w=(c,))
-    kz1 = ts(T.z1[:], T.h2[:, 32:33], T.c1[:], T.c3[:], A.mult, A.add)
-    V(scn, T.cs[:], T.one[:], T.fl[:], 0.0, A.mult, A.add, w=(kfl,))
-    kz2 = ts(T.z2[:], T.h2[:, 63:64], T.c2[:], T.z1[:], A.mult, A.add, w=(kz1,))
-    c = ts(T.dm[:], T.k256[:], T.cs[:, 31:32], T.z2[:], A.mult, A.add, w=(kz2,))
-    c = V(tr, T.dmt[:], T.dm[:], w=(c,))
-    c = V(rd, T.enc[:], T.dmt[:, 0:16], X, A.add, w=(c,))
-    ke16 = V(cp, T.e16[:, 0:1], T.enc[:], w=(c,))
+    kz1 = ts(T.z1[:], T.h2[:, 0:1], T.c1[:], T.c3[:], A.mult, A.add)
+    cs = T.cc[:, 0:32]
+    kcs = V(scn, cs, T.one[:], T.fl[:], T.c0[:], A.mult, A.add, w=(kfl,))
+    kz2 = ts(T.z2[:], T.h2[:, 31:32], T.c2[:], T.z1[:], A.mult, A.add, w=(kz1,))
+    c = ts(T.dm[:], T.kw[:], T.cc[:, 31:32], T.z2[:], A.mult, A.add, w=(kz2, kcs, kval))
+    knf = V(tt, T.nfe[:], here, prev, A.is_equal)
+    kdm = V(tr, T.dmt[:], T.dm[:], w=(c,))
+    knf = V(tt, T.nfd[:], T.nfe[:], T.trash[:], A.mult, w=(knf,))
+    ken = V(rd, T.enc[:], T.dmt[:], X, A.add, w=(kdm,))
+    ke16 = ts(T.e16[:, 0:1], T.enc[:], 256.0, None, A.mult, w=(ken,))
+    kcx = V(tt, T.cc[:, 32:64], cs, T.nfd[:], A.max, w=(knf,))
+    kfj = V(tt, T.fj[:], T.fl[:], T.j4[:], A.mult)
 
     arrive = {"e0": 0, "e1": 0, "e2": 0}
     for s in cores:
@@ -229,10 +258,9 @@ def rank_program(g, core, T, topo):
                                srcs=[T.e16[:, 0:1]], dsts=[T.m16[:, r:r + 1] for d in ds]) for e, ds in groups.items()],
             local_sem=T.sem.l0)
         cnt["l0"] = sum(len(e) for e in groups)
-    need("y", ke16)
-    da = load("y", T.at[:], T.a[:], "da")
-    dw = load("y", T.wt[:], T.w[:], "dw")
-    dv = load("y", T.vt[:], T.v[:], "dv")
+    if not ahead:
+        need("y", ("l0", cnt["l0"]))
+        da.append(load("y", T.at[:, 1024:2048], T.a[:, 1024:2048], "da1"))
 
     plan = _plan(core, cores, topo)
 
@@ -252,47 +280,42 @@ def rank_program(g, core, T, topo):
                 cnt[lsem] = cnt.get(lsem, 0) + len(es[part])
             g.remote_dma_fused(tl, local_sem=T.sem[lsem])
 
-    c = ts(T.dm2[:, 0:32], T.one[:], T.cs[:, 31:32], None, A.mult)
-    V(tt, T.nfe[:], here, prev, A.is_equal)
-    c2 = V(tt, T.fj[:], T.fl[:], T.j4[:], A.mult)
-    c = V(tr, T.dm2t[:, 0:32], T.dm2[:, 0:32], w=(c,))
-    V(rd, T.lj[:], T.fj[:], X, A.max, w=(c2,))
-    c = V(scn, T.iw[:, 1:17], T.one[:, 0:16], T.dm2t[:, 0:16], -1.0, A.mult, A.add, w=(c, kval))
-    for i in range(4):
-        V(tt, T.nfd[:, 16 * i:16 * i + 16], T.nfe[:, 16 * (i // 2):16 * (i // 2) + 16],
-          T.trash[:, 16 * (i // 2):16 * (i // 2) + 16], A.mult)
-    c = V(tr, T.ex[:], T.iw[:], w=(c,))
-    ts(T.dm2[:, 32:64], T.one[:], T.lj[:], None, A.mult)
-    for i in range(4):
-        c = ts(T.cd[:, 16 * i:16 * i + 16], T.cs[:, 16 * (i // 2):16 * (i // 2) + 16], T.ex[:, 0:1], None, A.add,
-               w=(c,) if i == 0 else ())
-    c = V(tt, T.od[:], T.cd[:], T.nfd[:], A.max, w=(c,))
-    c2 = V(tr, T.dm2t[:, 32:64], T.dm2[:, 32:64])
-    c = V(tr, T.to[:], T.od[:], w=(c,))
-    c2 = V(rd, T.last[:], T.dm2t[:, 32:48], X, A.max, w=(c2,))
-    klast = ts(T.lastl[:, 0:1], tcol, T.last[:], None, A.add, w=(c2,))
-    V(cp, T.offl[:, 0:32:2], T.to[:, 0:16], w=(c,))
-    c = V(cp, T.offl[:, 1:32:2], T.to[:, 32:48])
-    need("s", klast, kval, dx[0], dx[1], dx[2], dx[3])
+    V(scn, T.iw[:, 1:17], T.one[:, 0:16], T.dmt[:, 0:16], 0.0, A.mult, A.add, w=(kdm, kff))
+    kiw = V(tr, T.cct[:], T.cc[:], w=(kcx,))
+    klj = V(rd, T.lj[:], T.fj[:], X, A.max, w=(kfj,))
+    kof = V(tt, T.offf[:], T.cct[:, 32:48], T.iw[:, 0:16], A.add, w=(kiw,))
+    klj = ts(T.dm2[:], T.one[:], T.lj[:], None, A.mult, w=(klj,))
+    kof = V(cp, T.offl[:], T.offf[:], w=(kof,))
+    klj = V(tr, T.dm2t[:], T.dm2[:], w=(klj,))
+    if r:
+        V(cp, T.owni[:], T.e16[:, 0:1], w=(ke16,))
+    klj = V(rd, T.last[:], T.dm2t[:, 0:16], X, A.max, w=(klj,))
+    klast = ts(T.lastl[:, 0:1], tcol, T.last[:], None, A.add, w=(klj,))
+    c = V(cp, T.ff[:, 0:FW].indirect(T.offl[:]), T.val[:], w=(kof,))
+    need("s", klast, kff, dx[0], dx[1], dx[2], dx[3])
     if ahead:
-        klt = done(sca.activation(T.lt[:, 0:16], T.xs[:, 0:2048].indirect(T.lastl[:, 0:1]), AF.Copy), "ks")
+        klt = sc(T.lt[:, 0:16], T.xs[:, 0:2048].indirect(T.lastl[:, 0:1]))
         klt = V(qz, T.ql[:], T.sl[:], T.lt[:], w=(klt,))
         need("g", klt)
         exchange(T.ql, T.sl, {d: 0 for d in plan}, 2, 16, "e1", "l1")
     for b in range(N):
-        klb = done(sca.activation(T.ct[:, 72 * b + 64:72 * b + 80], T.xs[:, 0:2048].indirect(T.lastl[:, 0:1]), AF.Copy), "ks")
-    c = V(cp, T.ff[:, 0:FW].indirect(T.offl[:, 0:32]), T.val[:, 0:512], w=(c,))
-    if r:
-        V(cp, T.owni[:], T.enc[:])
+        klb = sc(T.ct[:, 72 * b + 64:72 * b + 80], T.xs[:, 0:2048].indirect(T.lastl[:, 0:1]))
     c = V(tt, T.mk[:], T.ff[:, 0:128].indirect(T.prm[:, 0:8]), T.msk[:], A.mult, w=(c,))
     if r:
-        ts(T.fi[:, r:r + 1], T.owni[:], 4, 15, A.logical_shift_right, A.bitwise_and, w=(c,))
+        ts(T.fi[:, r:r + 1], T.owni[:], 4, 15, A.logical_shift_right, A.bitwise_and)
     c = V(scn, T.sg[:], T.d0[:], T.mk[:], 0.0, A.mult, A.add, w=(c,))
-    c = ts(T.uu[:, 0:32], T.sg[:, 3:128:4], tcol, None, A.add, w=(c,))
-    c = V(cp, T.uu[:, 32:64], T.uu[:, 0:32], w=(c,))
-    c = V(cp, T.uu[:, 64:128], T.uu[:, 0:64], w=(c,))
-    V(cp, T.uu[:, 128:256], T.uu[:, 0:128], w=(c,))
-    kuu = V(cp, T.uu[:, 256:288], T.uu[:, 0:32])
+    c = ts(T.u0[:], T.sg[:, 3:128:4], T.th[:], None, A.add, w=(c,))
+    c = V(tr, T.ut[:], T.u0[:], w=(c,))
+    V(tt, T.us[:, 0:16], T.ut[:, 0:16], T.ut[:, 16:32], A.add, w=(c,))
+    c = V(tt, T.us[:, 16:32], T.ut[:, 0:16], T.ut[:, 16:32], A.add)
+    kuu = [V(tr, T.uu[:, 0:32], T.us[:], w=(c,))]
+    nb = min(r + 2, N)
+    for b in range(1, nb):
+        if b % 2:
+            kv = V(cp, T.uu[:, 32 * b:32 * b + 32], T.uu[:, 0:32], w=(kuu[0],))
+        else:
+            ks = sc(T.uu[:, 32 * b:32 * b + 32], T.uu[:, 0:32], w=(kuu[0],))
+    kuu = [kv] + ([ks] if nb > 2 else [])
 
     if r == 0:
         V(ms, T.nf0[:], 0.0)
@@ -310,44 +333,38 @@ def rank_program(g, core, T, topo):
         V(tt, T.ne[:, 0:r], T.fi[:, 1:r + 1], T.la[:, 0:r], A.not_equal, w=(c,))
         c = V(cp, T.c7f[:, 0:r], T.c7[:, 0:r], w=(c2,))
         c = V(scn, T.sb[:, 0:r], T.c7f[:, 0:r], T.ne[:, 0:r], 0.0, A.add, A.add, w=(c,))
-    c = ts(T.ro[:], T.rst[:], sb, -4.0, A.add, A.mult, w=(c, kuu))
-    klst = V(cp, T.lst[:], T.uu[:, 0:UW].indirect(T.ro[:, 0:2]), w=(c,))
+    c = ts(T.ro[:], T.rst[:], sb, -4.0, A.add, A.mult, w=(c,))
+    klst = V(cp, T.lst[:], T.uu[:, 0:32 * nb].indirect(T.ro[:, 0:2]), w=(c, *kuu))
     need("s", klst, klb)
-    for b in range(4, N):
-        kcs2 = done(sca.activation(T.ct[:, 72 * b:72 * b + 64], T.xs[:, 0:2048].indirect(T.lst[:, 4 * b:4 * b + 4]), AF.Copy), "ks")
-    for b in range(0, 4):
+    for b in range(5, N):
+        kcs2 = sc(T.ct[:, 72 * b:72 * b + 64], T.xs[:, 0:2048].indirect(T.lst[:, 4 * b:4 * b + 4]))
+    for b in range(0, 5):
         c = V(cp, T.ct[:, 72 * b:72 * b + 64], T.xs[:, 0:2048].indirect(T.lst[:, 4 * b:4 * b + 4]), w=(klst, klb))
     kqc = V(qz, T.qc[:, 0:NC], T.sc[:, 0:NC], T.ct[:, 0:4 * NC], w=(c, kcs2))
     need("g", kqc)
     exchange(T.qc, T.sc, {d: S * ((T.rank_of(d) - r - 1) % N) for d in plan}, 16 if ahead else S, 0, "e1", "l1")
+    if not ahead:
+        need("y", ("l1", cnt["l1"]))
+        dv = load("y", T.vt[:], T.v[:], "dv")
+        dw = load("y", T.wt[:], T.w[:], "dw")
 
     kqa = {}
     for i in range(4):
-        kqa[i] = V(qz, T.qa[:, 128 * i:128 * i + 128], T.sa[:, 128 * i:128 * i + 128], T.at[:, 512 * i:512 * i + 512], w=(da,))
-    kqv = V(qz, T.qv[:], T.sv[:], T.vt[:], w=(dv,))
-    kqw = V(qz, T.qw[:], T.sw[:], T.wt[:], w=(dw,))
-    need("t", kqw, *kqx.values())
-    kwx = done(ten.matmul_mx(T.ps[:, 1024:1536], T.qw[:], T.sw[:], T.qx[:], T.sx[:], True, True), "kt")
-    need("s", kwx)
-    kwxs = done(sca.activation(T.wx[:], T.ps[:, 1024:1536], AF.Copy), "ks")
+        kqa[i] = V(qz, T.qa[:, 128 * i:128 * i + 128], T.sa[:, 128 * i:128 * i + 128], T.at[:, 512 * i:512 * i + 512],
+                   w=(da[i // 2],))
+    kcd = V(tt, T.tcs[:], T.cct[:, 0:32], T.iw[:], A.add)
     if r:
         c = ts(T.ci[:, 0:r], T.mi[:, 0:r], 8, None, A.logical_shift_right)
         V(tt, T.nf0[:], T.fi[:, r:r + 1], T.la[:, r - 1:r], A.is_equal)
+    kcd = V(tr, T.cdw[:], T.tcs[:], w=(kcd,))
+    if r:
         c = V(cp, T.cif[:, 0:r], T.ci[:, 0:r], w=(c,))
-        V(scn, T.sbb[:, 0:r], T.cif[:, 0:r], T.ne[:, 0:r], 0.0, A.add, A.add, w=(c,))
     ts(T.lb0[:], here, -1.0, 16.0, A.mult, A.add)
-    c = V(tr, T.tc[:], T.cd[:])
-    ts(T.ii[:], T.tc[:], 0.125, -0.4375, A.mult, A.add, w=(c,))
-    c = ts(T.t1[:], T.tc[:], sb, float(N - r), A.add, A.add)
-    ts(T.fx[:], T.tc[:], 0.0, T.nf0[:], A.is_equal, A.mult)
-    c = ts(T.kk[:], T.t1[:], 7, None, A.bitwise_and, w=(c,))
-    ts(T.lb1[:, 0:16], T.cd[:, 0:16], sbb, None, A.add)
-    klb1 = ts(T.lb1[:, 16:32], T.cd[:, 32:48], sbb, None, A.add)
-    c = ts(T.k18[:], T.kk[:], float(S), 1.0, A.mult, A.add, w=(c,))
-    c = V(tt, T.s1[:], T.k18[:], T.ii[:], A.add, w=(c,))
-    c = V(tt, T.s2[:], T.s1[:], T.fx[:], A.subtract, w=(c,))
-    V(cp, T.fin[:, 0:32:2], T.s2[:, 0:16], w=(c,))
-    kfin = V(cp, T.fin[:, 1:32:2], T.s2[:, 32:48])
+    if r:
+        c = V(scn, T.sbb[:, 0:r], T.cif[:, 0:r], T.ne[:, 0:r], 0.0, A.add, A.add, w=(c,))
+    for i in range(4):
+        kcp = V(cp, T.cd[:, 16 * i:16 * i + 16], T.cdw[:, 16 * (i // 2):16 * (i // 2) + 16], w=(kcd,))
+    klb1 = ts(T.lb1[:], T.cdw[:], sbb, None, A.add, w=(c,))
     need("y", klb1)
     done(syn.dma_start(T.lb[0:1, :], T.lb0[0:16, :]), "dl0", 16)
     done(syn.dma_start(T.lb[1:2, :], T.lb1[0:16, :]), "dl1", 16)
@@ -360,7 +377,7 @@ def rank_program(g, core, T, topo):
         o = T.ps[:, 2048 + 512 * i:2048 + 512 * i + NC]
         m = done(ten.matmul_mx(o, T.qa[:, 128 * i:128 * i + 128], T.sa[:, 128 * i:128 * i + 128],
                                T.qc[:, NC - S:NC + 126], T.sc[:, NC - S:NC + 126], True, True), "kt")
-        if i % 2:
+        if i % 2 == 0:
             need("s", m)
             kh.append(done(sca.activation(T.ht[:, i:576:4], o, AF.Relu, 0.0, 0.05), "ks"))
         else:
@@ -369,21 +386,36 @@ def rank_program(g, core, T, topo):
     need("g", kqh)
     exchange(T.qh, T.sh, {d: S * ((T.rank_of(d) - r) % N) - 1 for d in plan}, S, 0, "e2", "l2")
 
+    c = V(tr, T.tc[:], T.cd[:], w=(kcp,))
+    ts(T.ii[:], T.tc[:], 0.125, -0.4375, A.mult, A.add, w=(c,))
+    c = ts(T.t1[:], T.tc[:], sb, float(N - r), A.add, A.add)
+    ts(T.fx[:], T.tc[:], 0.0, T.nf0[:], A.is_equal, A.mult)
+    c = ts(T.kk[:], T.t1[:], 7, None, A.bitwise_and, w=(c,))
+    kqv = V(qz, T.qv[:], T.sv[:], T.vt[:], w=(dv,))
     need("t", kqh, kqv)
     m = done(ten.matmul_mx(T.ps[:, 1536:1536 + NC], T.qv[:], T.sv[:], T.qh[:, 0:NC], T.sh[:, 0:NC], True, True), "kt")
+    c = ts(T.k18[:], T.kk[:], float(S), 1.0, A.mult, A.add, w=(c,))
+    kqw = V(qz, T.qw[:], T.sw[:], T.wt[:], w=(dw,))
+    need("t", kqw, *kqx.values())
+    kwx = done(ten.matmul_mx(T.ps[:, 1024:1536], T.qw[:], T.sw[:], T.qx[:], T.sx[:], True, True), "kt")
+    kwxs = sc(T.wx[:], T.ps[:, 1024:1536], w=(kwx,))
+    c = V(tt, T.s1[:], T.k18[:], T.ii[:], A.add, w=(c,))
     V(cp, T.vw[:, 0:1], T.ps[:, 1536 + NC - 2:1536 + NC - 1], w=(m,))
+    c = V(tt, T.s2[:], T.s1[:], T.fx[:], A.subtract, w=(c,))
     V(cp, T.vw[:, 1:S], T.ps[:, 1536:1536 + S - 1])
+    V(cp, T.fin[:, 0:32:2], T.s2[:, 0:16], w=(c,))
+    kfin = V(cp, T.fin[:, 1:32:2], T.s2[:, 32:48])
+
     need("t", ("e2", arrive["e2"]))
     cnt["e2"] = arrive["e2"]
     m = done(ten.matmul_mx(T.ps[:, 0:128], T.qv[:], T.sv[:], T.qh[:, NC - 2:NC + 126], T.sh[:, NC - 2:NC + 126], True, True), "kt")
     c = V(cp, T.vw[:, S:NC], T.ps[:, 2:128], w=(m,))
-    for h in (0, 1):
-        k = 256 * h
-        c = V(tt, T.yt[:, k:k + 256], T.vw[:, 0:NC].indirect(T.fin[:, 16 * h:16 * h + 16]), T.wx[:, k:k + 256], A.add,
+    for h, (k, e) in enumerate(((0, 128), (128, 320), (320, 512))):
+        c = V(tt, T.yt[:, k:e], T.vw[:, 0:NC].indirect(T.fin[:, k // 16:e // 16]), T.wx[:, k:e], A.add,
               w=(c, kwxs, kfin) if h == 0 else ())
-        qn = "ys"[h]
+        qn = "ysy"[h]
         need(qn, c)
-        done(queue[qn].dma_start(T.y[:, k:k + 256], T.yt[:, k:k + 256]), "dy%d" % h, 16)
+        done(queue[qn].dma_start(T.y[:, k:e], T.yt[:, k:e]), "dy%d" % h, 16)
 
     for s in SEMAPHORES:
         if cnt.get(s):

from concourse.bass import DstId, RemoteDMATransfer
from concourse.mybir import dt, AluOpType, AxisListType, ActivationFunctionType

N = 8
S = 18
NC = N * S
ROOM = 160
FW = ROOM + 512 + 128
UW = N * 32

F32, BF, I32, U16, C8, U8 = "float32", "bfloat16", "int32", "uint16", "float8_e4m3fn_x4", "uint8"


def _sb(n, d):
    return ("sbuf", [128, n], d)


SCRATCH = {
    "ps": ("psum", [128, 4096], F32),
    "xs": _sb(2048, BF), "pt": _sb(576, BF), "at": _sb(2048, BF), "wt": _sb(512, BF), "vt": _sb(512, BF),
    "qx": _sb(512, C8), "sx": _sb(512, U8), "qp": _sb(144, C8), "sp": _sb(144, U8),
    "qa": _sb(512, C8), "sa": _sb(512, U8), "qw": _sb(128, C8), "sw": _sb(128, U8), "qv": _sb(128, C8), "sv": _sb(128, U8),
    "ct": _sb(592, BF), "qc": _sb(NC + 126, C8), "sc": _sb(NC + 126, U8), "lt": _sb(512, BF), "ql": _sb(128, C8),
    "sl": _sb(128, U8), "ht": _sb(576, BF), "qh": _sb(NC + 126, C8), "sh": _sb(NC + 126, U8),
    "pi": _sb(1, I32), "pj": _sb(4, I32), "pf": _sb(4, F32), "j4i": _sb(32, I32), "j4m": _sb(32, I32), "j4": _sb(32, F32),
    "trash": _sb(32, F32), "vali": _sb(256, F32), "val": _sb(256, F32), "prmi": _sb(8, I32), "prm": _sb(8, U16),
    "ypi": _sb(128, I32), "msk": _sb(128, F32), "d0": _sb(128, F32), "c0": _sb(1, F32), "c1": _sb(1, F32),
    "c2": _sb(1, F32), "c3": _sb(1, F32), "kr": _sb(1, F32), "th": _sb(1, F32), "lane": _sb(1, F32), "g64": _sb(1, F32),
    "rst": _sb(2, F32), "reset": _sb(128, F32), "one2": _sb(128, BF), "one": _sb(32, F32), "kw": _sb(32, F32),
    "z": _sb(288, F32), "mx": _sb(256, F32), "nn": _sb(256, BF), "ss": _sb(256, BF), "gg": _sb(64, F32), "h2": _sb(64, F32),
    "fl": _sb(32, F32), "cc": _sb(64, F32), "cct": _sb(64, F32), "z1": _sb(1, F32), "z2": _sb(1, F32), "dm": _sb(32, F32),
    "dmt": _sb(32, F32), "enc": _sb(1, F32), "e16": _sb(2, U16), "owni": _sb(1, I32),
    "fj": _sb(32, F32), "lj": _sb(1, F32), "dm2": _sb(32, F32), "dm2t": _sb(32, F32), "last": _sb(1, F32),
    "lastl": _sb(2, U16), "iw": _sb(32, F32), "nfe": _sb(32, F32), "nfd": _sb(32, F32),
    "offf": _sb(16, F32), "offl": _sb(16, U16), "ff": _sb(FW, F32),
    "mk": _sb(128, F32), "sg": _sb(128, F32), "u0": _sb(32, F32), "ut": _sb(32, F32), "us": _sb(32, F32), "uu": _sb(UW, F32),
    "m16": _sb(8, U16), "mi": _sb(8, I32), "fi": _sb(8, I32), "la": _sb(8, I32), "c7": _sb(8, I32), "c7f": _sb(8, F32),
    "ne": _sb(8, F32), "sb": _sb(8, F32), "ci": _sb(8, I32), "cif": _sb(8, F32), "sbb": _sb(8, F32), "nf0": _sb(1, F32),
    "ro": _sb(2, U16), "lst": _sb(32, U16),
    "tcs": _sb(32, F32), "cdw": _sb(32, F32), "cd": _sb(64, F32),
    "tc": _sb(64, F32), "ii": _sb(64, I32), "t1": _sb(64, I32), "kk": _sb(64, I32), "k18": _sb(64, F32), "fx": _sb(64, F32),
    "s1": _sb(64, F32), "s2": _sb(64, F32), "fin": _sb(32, U16), "lb0": _sb(32, F32), "lb1": _sb(32, F32),
    "wx": _sb(512, F32), "vw": _sb(NC, F32), "yt": _sb(512, F32),
}
SEMAPHORES = ["kv", "ks", "kt", "kg", "dp", "dx0", "dx1", "dx2", "dx3", "da0", "da1", "dw", "dv", "dy0", "dy1", "dy2",
              "dl0", "dl1", "e0", "e1", "e2", "l0", "l1", "l2"]


def _mask(es):
    return sum(1 << e for e in es)


def _near(core, d, off_engines, topo):
    return [e for e in topo.engines(core, d) if e not in off_engines][:2]


def _plan(core, cores, topo):
    ch = topo.chip(core)
    off = [d for d in cores if topo.chip(d) != ch]
    off.sort(key=lambda d: (0 if topo.mates(ch, topo.chip(d)) else 1 if topo.same_plane(ch, topo.chip(d)) else 2, d))
    eo = topo.engines(core, off[0])
    plan = {}
    for i, d in enumerate(off):
        j = 4 * (i - 4)
        plan[d] = ([eo[2 * i]], [eo[2 * i + 1]]) if i < 4 else (eo[j + 1:j + 4:2], eo[j:j + 4:2])
    for d in cores:
        if d != core and topo.chip(d) == ch:
            plan[d] = (_near(core, d, eo, topo),) * 2
    return plan


def _plan0(core, cores, topo):
    ch = topo.chip(core)
    eo = [topo.engines(core, d) for d in cores if topo.chip(d) != ch][0]
    return {d: eo if topo.chip(d) != ch else _near(core, d, eo, topo) for d in cores[cores.index(core) + 1:]}


def _ahead(core, cores, topo):
    return all(topo.chip(d) == topo.chip(core) for d in cores[cores.index(core) + 1:])


def rank_program(g, core, T, topo):
    r = T.rank_of(core)
    if r is None:
        return
    A, X, AF = AluOpType, AxisListType.X, ActivationFunctionType
    cores = list(T.cores)
    vec, sca, ten, syn = g.vector, g.scalar, g.tensor, g.sync
    queue = {"v": vec, "s": sca, "t": ten, "g": g, "y": syn}
    cnt, known = {}, {}

    def done(ins, sem, n=1):
        ins.then_inc(T.sem[sem], n)
        cnt[sem] = cnt.get(sem, 0) + n
        return (sem, cnt[sem])

    def need(qn, *toks):
        for s, v in toks:
            if known.get((qn, s), 0) < v:
                queue[qn].wait_ge(T.sem[s], v)
                known[(qn, s)] = v

    def V(f, *args, w=()):
        need("v", *w)
        return done(f(*args), "kv")

    def ts(out, i, a, b, o0, o1=None, w=()):
        need("v", *w)
        if o1 is None:
            return done(vec.tensor_scalar(out, i, a, None, o0), "kv")
        return done(vec.tensor_scalar(out, i, a, b, o0, o1), "kv")

    def io(out, pattern, base, cm):
        return done(g.iota(out, pattern, base, cm, allow_small_or_imprecise_dtypes=True), "kg")

    def sc(out, in_, w=()):
        need("s", *w)
        return done(sca.activation(out, in_, AF.Copy), "ks")

    def si(out, in_, bias, scale, w=()):
        need("s", *w)
        return done(sca.activation(out, in_, AF.Identity, bias, scale), "ks")

    tt, cp, ms, rd, scn, tr, qz = (vec.tensor_tensor, vec.tensor_copy, vec.memset, vec.tensor_reduce,
                                   vec.tensor_tensor_scan, vec.transpose, vec.quantize_mx)

    def load(qn, out, in_, sem):
        return done(queue[qn].dma_start(out, in_), sem, 16)

    dx = {}
    dx[0] = load("y", T.xs[:, 0:512], T.x[:, 0:512], "dx0")
    dp = load("s", T.pt[:, 0:128], T.p[:, 0:128], "dp")
    dx[2] = load("s", T.xs[:, 1024:1536], T.x[:, 1024:1536], "dx2")
    dx[1] = load("y", T.xs[:, 512:1024], T.x[:, 512:1024], "dx1")
    dx[3] = load("s", T.xs[:, 1536:2048], T.x[:, 1536:2048], "dx3")
    da = [load("s", T.at[:, 0:1024], T.a[:, 0:1024], "da0")]
    ahead = _ahead(core, cores, topo)
    if ahead:
        da.append(load("s", T.at[:, 1024:2048], T.a[:, 1024:2048], "da1"))
        dv = load("s", T.vt[:], T.v[:], "dv")
        dw = load("s", T.wt[:], T.w[:], "dw")

    kpi = io(T.pi[:], [[1, 1]], 0, 1)
    kj4 = io(T.j4i[:], [[4, 32]], 0, 128)
    kone = io(T.one[:], [[0, 32]], 1, 0)
    kypi = io(T.ypi[:], [[0, 32], [1, 4]], 0, 0)
    kprm = io(T.prmi[:], [[1, 8]], 0, 8)
    kgg = io(T.gg[:], [[0, 64]], 0, 0)
    io(T.z[:, 24:32], [[0, 8]], 0, 0)
    kc = io(T.one2[:], [[0, 128]], 1, 0)
    kval = io(T.vali[:], [[128, 16], [4, 16]], 0, 0)
    io(T.iw[:], [[0, 32]], 0, 0)
    kff = io(T.ff[:, 0:ROOM], [[0, ROOM]], 0, 0)
    if ahead:
        kff = io(T.lt[:], [[0, 512]], 0, 0)
    c = V(ms, T.reset[:], 0.0)
    ts(T.pj[:, 0:1], T.pi[:], 31, None, A.bitwise_and, w=(kpi,))
    ts(T.pj[:, 1:2], T.pi[:], 15, None, A.bitwise_and)
    ts(T.pj[:, 2:3], T.pi[:], 3, None, A.bitwise_and)
    c2 = ts(T.pj[:, 3:4], T.pi[:], 2, 3, A.logical_shift_right, A.bitwise_and)
    V(ms, T.reset[:, 0:128:16], -5e29, w=(c,))
    cpf = V(cp, T.pf[:], T.pj[:], w=(c2,))
    c = ts(T.j4m[:], T.j4i[:], 4095, None, A.bitwise_and, w=(kj4,))
    ckr = ts(T.kr[:], T.pf[:, 0:1], 16.0, None, A.is_lt, w=(cpf,))
    cg = V(tt, T.lane[:], T.pf[:, 0:1], T.pf[:, 1:2], A.subtract)
    cj4 = V(cp, T.j4[:], T.j4m[:], w=(c,))
    ts(T.c0[:], T.pf[:, 0:1], 0.0, -1.0, A.is_equal, A.mult)
    ts(T.c1[:], T.pf[:, 0:1], 17.0, 16.0 / 256, A.is_equal, A.mult)
    ts(T.c3[:], T.pf[:, 0:1], 17.0, -17.0 / 256, A.is_equal, A.mult)
    ts(T.c2[:], T.pf[:, 0:1], 16.0, 1.0 / 256, A.is_equal, A.mult)
    tcol, rho = T.pf[:, 2:3], T.pf[:, 3:4]
    ts(T.msk[:], T.ypi[:], rho, None, A.is_equal, w=(kypi,))
    ts(T.d0[:], T.ypi[:], 0.0, None, A.not_equal)
    c2 = ts(T.prmi[:], T.prmi[:], 127, None, A.bitwise_and, w=(kprm,))
    V(ms, T.gg[:, 0:1], 99.0, w=(kgg,))
    V(cp, T.prm[:], T.prmi[:], w=(c2,))
    turn = 4.0 * ((r + 1) % N) + 4.0 * N * r
    si(T.th[:], T.pf[:, 2:3], 0.0, 0.5, w=(cpf,))
    si(T.rst[:, 0:1], T.pf[:, 1:2], -0.25 * turn, -0.25)
    si(T.rst[:, 1:2], T.pf[:, 1:2], -0.25 * (turn + 16.0), -0.25)
    need("s", kone, ckr)
    si(T.kw[:], T.one[:], 0.0, T.kr[:])
    kg64 = si(T.g64[:], T.lane[:], 0.0, 4.0, w=(cg,))
    si(T.trash[:], T.j4[:], float(ROOM), 0.25, w=(cj4,))
    kval = si(T.val[:], T.vali[:], T.g64[:], 1.0, w=(kval, kg64))

    c = V(cp, T.pt[:, 128:256], T.pt[:, 0:128], w=(dp,))
    V(cp, T.pt[:, 512:576], T.pt[:, 0:64])
    c = V(cp, T.pt[:, 256:512], T.pt[:, 0:256], w=(c,))
    kqp = V(qz, T.qp[:], T.sp[:], T.pt[:], w=(c,))

    kqx, ksc, kch = {}, {}, {}

    def pack(i):
        b, h = i % 2, i // 2
        kqx[i] = V(qz, T.qx[:, 128 * i:128 * i + 128], T.sx[:, 128 * i:128 * i + 128], T.xs[:, 512 * i:512 * i + 512],
                   w=(dx[i],))
        need("t", kqp, kqx[i])
        ksc[b] = done(ten.matmul_mx(T.ps[:, 512 * b:512 * b + 128], T.qp[:, 16 * h:16 * h + 128],
                                    T.sp[:, 16 * h:16 * h + 128], T.qx[:, 128 * i:128 * i + 128],
                                    T.sx[:, 128 * i:128 * i + 128], h == 0, h == 1), "kt")

    def step(b, n):
        k = slice(128 * b, 128 * b + 128)
        z, before = T.z[:, 32 + 128 * b:160 + 128 * b], T.z[:, 31 + 128 * b:159 + 128 * b]
        if n == 0:
            kch[b] = V(tr, z, T.ps[:, 512 * b:512 * b + 128], w=(ksc[b],))
        elif n == 1:
            kch[b] = V(scn, T.mx[:, k], before, T.reset[:], 0.0, A.max, A.add, w=(kch[b], kc))
        elif n == 2:
            kch[b] = V(tt, T.nn[:, k], z, T.mx[:, k], A.is_le, w=(kch[b],))
        else:
            kch[b] = V(scn, T.ss[:, k], T.nn[:, k], T.one2[:], 0.0, A.mult, A.add, w=(kch[b],))
        return kch[b]

    pack(0), pack(2), step(0, 0), step(0, 1), pack(1), pack(3), step(0, 2), step(1, 0), step(0, 3), step(1, 1)
    V(cp, T.gg[:, 17:18], T.ss[:, 15:16], w=(kch[0],))
    step(1, 2)
    c = step(1, 3)
    for h in (0, 1):
        V(cp, T.gg[:, 1 + 8 * h:9 + 8 * h], T.ss[:, 16 * h + 15:256:32], w=(c,))
        c2 = V(cp, T.gg[:, 32 + 8 * h:40 + 8 * h], T.ss[:, 16 * h + 15:256:32])
    c = V(tr, T.h2[:], T.gg[:], w=(c2,))
    here, prev = T.h2[:, 32:64], T.h2[:, 31:63]
    kfl = V(tt, T.fl[:], here, prev, A.not_equal, w=(c,))
    kz1 = ts(T.z1[:], T.h2[:, 0:1], T.c1[:], T.c3[:], A.mult, A.add)
    cs = T.cc[:, 0:32]
    kcs = V(scn, cs, T.one[:], T.fl[:], T.c0[:], A.mult, A.add, w=(kfl,))
    kz2 = ts(T.z2[:], T.h2[:, 31:32], T.c2[:], T.z1[:], A.mult, A.add, w=(kz1,))
    c = ts(T.dm[:], T.kw[:], T.cc[:, 31:32], T.z2[:], A.mult, A.add, w=(kz2, kcs, kval))
    knf = V(tt, T.nfe[:], here, prev, A.is_equal)
    kdm = V(tr, T.dmt[:], T.dm[:], w=(c,))
    knf = V(tt, T.nfd[:], T.nfe[:], T.trash[:], A.mult, w=(knf,))
    ken = V(rd, T.enc[:], T.dmt[:], X, A.add, w=(kdm,))
    ke16 = ts(T.e16[:, 0:1], T.enc[:], 256.0, None, A.mult, w=(ken,))
    kcx = V(tt, T.cc[:, 32:64], cs, T.nfd[:], A.max, w=(knf,))
    kfj = V(tt, T.fj[:], T.fl[:], T.j4[:], A.mult)

    arrive = {"e0": 0, "e1": 0, "e2": 0}
    for s in cores:
        if s != core:
            n = sum(len(es) for es in _plan(s, cores, topo)[core])
            arrive["e0"] += len(_plan0(s, cores, topo).get(core, []))
            arrive["e1"] += n * (2 if _ahead(s, cores, topo) else 1)
            arrive["e2"] += n

    def did(d):
        rid, pid, _ = topo.addr(d)
        return DstId(rid=rid, pnc=pid)

    groups = {}
    for d, e in _plan0(core, cores, topo).items():
        groups.setdefault(tuple(e), []).append(d)
    if groups:
        need("g", ke16)
        g.remote_dma_fused(
            [RemoteDMATransfer(dst_ids=[did(d) for d in ds], dma_engine_mask=_mask(e), remote_sem=T.sem.e0,
                               srcs=[T.e16[:, 0:1]], dsts=[T.m16[:, r:r + 1] for d in ds]) for e, ds in groups.items()],
            local_sem=T.sem.l0)
        cnt["l0"] = sum(len(e) for e in groups)
    if not ahead:
        need("y", ("l0", cnt["l0"]))
        da.append(load("y", T.at[:, 1024:2048], T.a[:, 1024:2048], "da1"))

    plan = _plan(core, cores, topo)

    def exchange(codes, plane, first, width, at, rsem, lsem):
        land = (T.qc, T.sc) if rsem == "e1" else (T.qh, T.sh)
        for part in (0, 1):
            tl = []
            for d, es in plan.items():
                k = first[d]
                slot = NC + S * (((r - T.rank_of(d)) % N) - 1) + at
                if part == 0:
                    src, dst = codes[:, k:k + width].bitcast(dt.uint8), land[0][:, slot:slot + width].bitcast(dt.uint8)
                else:
                    src, dst = plane[:, k:k + width], land[1][:, slot:slot + width]
                tl.append(RemoteDMATransfer(dst_ids=[did(d)], dma_engine_mask=_mask(es[part]), remote_sem=T.sem[rsem],
                                            srcs=[src], dsts=[dst]))
                cnt[lsem] = cnt.get(lsem, 0) + len(es[part])
            g.remote_dma_fused(tl, local_sem=T.sem[lsem])

    V(scn, T.iw[:, 1:17], T.one[:, 0:16], T.dmt[:, 0:16], 0.0, A.mult, A.add, w=(kdm, kff))
    kiw = V(tr, T.cct[:], T.cc[:], w=(kcx,))
    klj = V(rd, T.lj[:], T.fj[:], X, A.max, w=(kfj,))
    kof = V(tt, T.offf[:], T.cct[:, 32:48], T.iw[:, 0:16], A.add, w=(kiw,))
    klj = ts(T.dm2[:], T.one[:], T.lj[:], None, A.mult, w=(klj,))
    kof = V(cp, T.offl[:], T.offf[:], w=(kof,))
    klj = V(tr, T.dm2t[:], T.dm2[:], w=(klj,))
    if r:
        V(cp, T.owni[:], T.e16[:, 0:1], w=(ke16,))
    klj = V(rd, T.last[:], T.dm2t[:, 0:16], X, A.max, w=(klj,))
    klast = ts(T.lastl[:, 0:1], tcol, T.last[:], None, A.add, w=(klj,))
    c = V(cp, T.ff[:, 0:FW].indirect(T.offl[:]), T.val[:], w=(kof,))
    need("s", klast, kff, dx[0], dx[1], dx[2], dx[3])
    if ahead:
        klt = sc(T.lt[:, 0:16], T.xs[:, 0:2048].indirect(T.lastl[:, 0:1]))
        klt = V(qz, T.ql[:], T.sl[:], T.lt[:], w=(klt,))
        need("g", klt)
        exchange(T.ql, T.sl, {d: 0 for d in plan}, 2, 16, "e1", "l1")
    for b in range(N):
        klb = sc(T.ct[:, 72 * b + 64:72 * b + 80], T.xs[:, 0:2048].indirect(T.lastl[:, 0:1]))
    c = V(tt, T.mk[:], T.ff[:, 0:128].indirect(T.prm[:, 0:8]), T.msk[:], A.mult, w=(c,))
    if r:
        ts(T.fi[:, r:r + 1], T.owni[:], 4, 15, A.logical_shift_right, A.bitwise_and)
    c = V(scn, T.sg[:], T.d0[:], T.mk[:], 0.0, A.mult, A.add, w=(c,))
    c = ts(T.u0[:], T.sg[:, 3:128:4], T.th[:], None, A.add, w=(c,))
    c = V(tr, T.ut[:], T.u0[:], w=(c,))
    V(tt, T.us[:, 0:16], T.ut[:, 0:16], T.ut[:, 16:32], A.add, w=(c,))
    c = V(tt, T.us[:, 16:32], T.ut[:, 0:16], T.ut[:, 16:32], A.add)
    kuu = [V(tr, T.uu[:, 0:32], T.us[:], w=(c,))]
    nb = min(r + 2, N)
    for b in range(1, nb):
        if b % 2:
            kv = V(cp, T.uu[:, 32 * b:32 * b + 32], T.uu[:, 0:32], w=(kuu[0],))
        else:
            ks = sc(T.uu[:, 32 * b:32 * b + 32], T.uu[:, 0:32], w=(kuu[0],))
    kuu = [kv] + ([ks] if nb > 2 else [])

    if r == 0:
        V(ms, T.nf0[:], 0.0)
        sb = sbb = T.sb[:, 0:1]
        c = V(ms, sb, 0.0)
    else:
        need("v", ("e0", arrive["e0"]))
        cnt["e0"] = arrive["e0"]
        sb, sbb = T.sb[:, r - 1:r], T.sbb[:, r - 1:r]
        c = V(cp, T.mi[:, 0:r], T.m16[:, 0:r])
        if r > 1:
            ts(T.fi[:, 1:r], T.mi[:, 1:r], 4, 15, A.logical_shift_right, A.bitwise_and, w=(c,))
        c = ts(T.la[:, 0:r], T.mi[:, 0:r], 15, None, A.bitwise_and, w=(c,))
        c2 = ts(T.c7[:, 0:r], T.mi[:, 0:r], 8, 7, A.logical_shift_right, A.bitwise_and)
        V(tt, T.ne[:, 0:r], T.fi[:, 1:r + 1], T.la[:, 0:r], A.not_equal, w=(c,))
        c = V(cp, T.c7f[:, 0:r], T.c7[:, 0:r], w=(c2,))
        c = V(scn, T.sb[:, 0:r], T.c7f[:, 0:r], T.ne[:, 0:r], 0.0, A.add, A.add, w=(c,))
    c = ts(T.ro[:], T.rst[:], sb, -4.0, A.add, A.mult, w=(c,))
    klst = V(cp, T.lst[:], T.uu[:, 0:32 * nb].indirect(T.ro[:, 0:2]), w=(c, *kuu))
    need("s", klst, klb)
    for b in range(5, N):
        kcs2 = sc(T.ct[:, 72 * b:72 * b + 64], T.xs[:, 0:2048].indirect(T.lst[:, 4 * b:4 * b + 4]))
    for b in range(0, 5):
        c = V(cp, T.ct[:, 72 * b:72 * b + 64], T.xs[:, 0:2048].indirect(T.lst[:, 4 * b:4 * b + 4]), w=(klst, klb))
    kqc = V(qz, T.qc[:, 0:NC], T.sc[:, 0:NC], T.ct[:, 0:4 * NC], w=(c, kcs2))
    need("g", kqc)
    exchange(T.qc, T.sc, {d: S * ((T.rank_of(d) - r - 1) % N) for d in plan}, 16 if ahead else S, 0, "e1", "l1")
    if not ahead:
        need("y", ("l1", cnt["l1"]))
        dv = load("y", T.vt[:], T.v[:], "dv")
        dw = load("y", T.wt[:], T.w[:], "dw")

    kqa = {}
    for i in range(4):
        kqa[i] = V(qz, T.qa[:, 128 * i:128 * i + 128], T.sa[:, 128 * i:128 * i + 128], T.at[:, 512 * i:512 * i + 512],
                   w=(da[i // 2],))
    kcd = V(tt, T.tcs[:], T.cct[:, 0:32], T.iw[:], A.add)
    if r:
        c = ts(T.ci[:, 0:r], T.mi[:, 0:r], 8, None, A.logical_shift_right)
        V(tt, T.nf0[:], T.fi[:, r:r + 1], T.la[:, r - 1:r], A.is_equal)
    kcd = V(tr, T.cdw[:], T.tcs[:], w=(kcd,))
    if r:
        c = V(cp, T.cif[:, 0:r], T.ci[:, 0:r], w=(c,))
    ts(T.lb0[:], here, -1.0, 16.0, A.mult, A.add)
    if r:
        c = V(scn, T.sbb[:, 0:r], T.cif[:, 0:r], T.ne[:, 0:r], 0.0, A.add, A.add, w=(c,))
    for i in range(4):
        kcp = V(cp, T.cd[:, 16 * i:16 * i + 16], T.cdw[:, 16 * (i // 2):16 * (i // 2) + 16], w=(kcd,))
    klb1 = ts(T.lb1[:], T.cdw[:], sbb, None, A.add, w=(c,))
    need("y", klb1)
    done(syn.dma_start(T.lb[0:1, :], T.lb0[0:16, :]), "dl0", 16)
    done(syn.dma_start(T.lb[1:2, :], T.lb1[0:16, :]), "dl1", 16)

    need("t", ("e1", arrive["e1"]), kqc)
    cnt["e1"] = arrive["e1"]
    kh = []
    for i in range(4):
        need("t", kqa[i])
        o = T.ps[:, 2048 + 512 * i:2048 + 512 * i + NC]
        m = done(ten.matmul_mx(o, T.qa[:, 128 * i:128 * i + 128], T.sa[:, 128 * i:128 * i + 128],
                               T.qc[:, NC - S:NC + 126], T.sc[:, NC - S:NC + 126], True, True), "kt")
        if i % 2 == 0:
            need("s", m)
            kh.append(done(sca.activation(T.ht[:, i:576:4], o, AF.Relu, 0.0, 0.05), "ks"))
        else:
            kh.append(ts(T.ht[:, i:576:4], o, 0.0, 0.05, A.max, A.mult, w=(m,)))
    kqh = V(qz, T.qh[:, 0:NC], T.sh[:, 0:NC], T.ht[:], w=kh)
    need("g", kqh)
    exchange(T.qh, T.sh, {d: S * ((T.rank_of(d) - r) % N) - 1 for d in plan}, S, 0, "e2", "l2")

    c = V(tr, T.tc[:], T.cd[:], w=(kcp,))
    ts(T.ii[:], T.tc[:], 0.125, -0.4375, A.mult, A.add, w=(c,))
    c = ts(T.t1[:], T.tc[:], sb, float(N - r), A.add, A.add)
    ts(T.fx[:], T.tc[:], 0.0, T.nf0[:], A.is_equal, A.mult)
    c = ts(T.kk[:], T.t1[:], 7, None, A.bitwise_and, w=(c,))
    kqv = V(qz, T.qv[:], T.sv[:], T.vt[:], w=(dv,))
    need("t", kqh, kqv)
    m = done(ten.matmul_mx(T.ps[:, 1536:1536 + NC], T.qv[:], T.sv[:], T.qh[:, 0:NC], T.sh[:, 0:NC], True, True), "kt")
    c = ts(T.k18[:], T.kk[:], float(S), 1.0, A.mult, A.add, w=(c,))
    kqw = V(qz, T.qw[:], T.sw[:], T.wt[:], w=(dw,))
    need("t", kqw, *kqx.values())
    kwx = done(ten.matmul_mx(T.ps[:, 1024:1536], T.qw[:], T.sw[:], T.qx[:], T.sx[:], True, True), "kt")
    kwxs = sc(T.wx[:], T.ps[:, 1024:1536], w=(kwx,))
    c = V(tt, T.s1[:], T.k18[:], T.ii[:], A.add, w=(c,))
    V(cp, T.vw[:, 0:1], T.ps[:, 1536 + NC - 2:1536 + NC - 1], w=(m,))
    c = V(tt, T.s2[:], T.s1[:], T.fx[:], A.subtract, w=(c,))
    V(cp, T.vw[:, 1:S], T.ps[:, 1536:1536 + S - 1])
    V(cp, T.fin[:, 0:32:2], T.s2[:, 0:16], w=(c,))
    kfin = V(cp, T.fin[:, 1:32:2], T.s2[:, 32:48])

    need("t", ("e2", arrive["e2"]))
    cnt["e2"] = arrive["e2"]
    m = done(ten.matmul_mx(T.ps[:, 0:128], T.qv[:], T.sv[:], T.qh[:, NC - 2:NC + 126], T.sh[:, NC - 2:NC + 126], True, True), "kt")
    c = V(cp, T.vw[:, S:NC], T.ps[:, 2:128], w=(m,))
    for h, (k, e) in enumerate(((0, 128), (128, 320), (320, 512))):
        c = V(tt, T.yt[:, k:e], T.vw[:, 0:NC].indirect(T.fin[:, k // 16:e // 16]), T.wx[:, k:e], A.add,
              w=(c, kwxs, kfin) if h == 0 else ())
        qn = "ysy"[h]
        need(qn, c)
        done(queue[qn].dma_start(T.y[:, k:e], T.yt[:, k:e]), "dy%d" % h, 16)

    for s in SEMAPHORES:
        if cnt.get(s):
            need("g", (s, cnt[s]))
